import numpy as np
import ml_dtypes


def mxq(x, axis, fmt="e4m3"):
    dtype, down = {"e4m3": (ml_dtypes.float8_e4m3fn, 7), "e5m2": (ml_dtypes.float8_e5m2, 14)}[fmt]
    v = np.moveaxis(np.asarray(x, np.float32).astype(ml_dtypes.bfloat16).astype(np.float64), axis, -1)
    blocks = v.reshape(v.shape[:-1] + (-1, 32))
    amax = np.abs(blocks).max(-1, keepdims=True)
    byte = np.maximum(np.where(amax > 0, np.frexp(amax)[1] - 1 + 127, 0) - down, 1)
    scale = np.exp2(byte - 127.0)
    codes = (blocks / scale).astype(np.float32).astype(dtype).astype(np.float64)
    return np.moveaxis((codes * scale).reshape(v.shape), -1, axis)


WIDE = False


def mx_kscale(k):
    if not WIDE:
        return np.ones(k)
    levels = np.array([10, -10, 5, -5, 0])
    if k % 512:
        return np.exp2(np.random.permutation(np.resize(levels, k // 32))).repeat(32)
    a = np.empty((k // 512, 16))
    for p in range(k // 512):
        a[p, :8] = np.random.permutation(np.resize(levels, 8))
        for g in range(8):
            far = levels[np.abs(levels - a[p, g]) >= 10]
            a[p, g + 8] = far[np.random.randint(len(far))]
    return np.exp2(a.ravel()).repeat(32)


BF16 = ml_dtypes.bfloat16


def bf(x):
    return np.asarray(x, np.float32).astype(BF16)


def f64(x):
    return np.asarray(x).astype(np.float64)


E2M1 = np.array([0.0, 0.5, 1.0, 1.5, 2.0, 3.0, 4.0, 6.0, -0.0, -0.5, -1.0, -1.5, -2.0, -3.0, -4.0, -6.0])


def pack_weight(w, fmt):
    k, n = w.shape
    w = f64(bf(w)).reshape(k // 32, 32, n)
    amax = np.abs(w).max(1)
    if fmt == "e4m3":
        byte = np.frexp(amax)[1] - 1 + 127 - 7
    else:
        mant, ex = np.frexp(amax / 6.0)
        byte = np.where(mant > 0.5, ex, ex - 1) + 127
    byte = np.clip(np.where(amax > 0, byte, 1), 1, 254)
    scaled = (w * np.exp2(127.0 - byte)[:, None, :]).reshape(k, n).astype(np.float32)
    by_word = np.ascontiguousarray(scaled.reshape(k // 512, 128, 4, n).transpose(0, 1, 3, 2))
    if fmt == "e4m3":
        words = by_word.astype(ml_dtypes.float8_e4m3fn).view(np.uint8)
    else:
        c = by_word.astype(ml_dtypes.float4_e2m1fn).view(np.uint8) & 0xF
        words = c[..., 0::2] | (c[..., 1::2] << 4)
    return np.ascontiguousarray(words), np.ascontiguousarray(byte.astype(np.uint8).reshape(k // 512, 16, n))


def unpack_weight(words, scales, fmt):
    g, p, n, _ = words.shape
    if fmt == "e4m3":
        vals = np.ascontiguousarray(words).view(ml_dtypes.float8_e4m3fn).astype(np.float64)
    else:
        nib = np.empty((g, p, n, 4), np.uint8)
        nib[..., 0::2] = words & 0xF
        nib[..., 1::2] = words >> 4
        vals = E2M1[nib]
    vals = vals * np.repeat(np.exp2(scales.astype(np.float64) - 127.0), 8, axis=1)[..., None]
    return vals.transpose(0, 1, 3, 2).reshape(g * 512, n)
def pack4(w):
    words, scales = pack_weight(w, "e2m1")
    return words.reshape(words.shape[0], 128, -1), scales


def unpack4(words, scales):
    return unpack_weight(words.reshape(words.shape[0], 128, -1, 2), scales, "e2m1")


E4M3FN = np.array([(-1.0 if i & 128 else 1.0) * ((1.0 + (i & 7) / 8.0) * 2.0 ** (((i >> 3) & 15) - 7) if i & 120 else (i & 7) * 2.0 ** -9) for i in range(256)])


def e4m3fn_bytes(y):
    return np.clip(np.asarray(y, np.float64), -448.0, 448.0).astype(np.float32).astype(ml_dtypes.float8_e4m3fn).view(np.uint8)


def e4m3fn_values(b):
    return E4M3FN[b]


N, M, E, H, W = 128, 128, 512, 1024, 256
G = 3 * H


def sigmoid(v):
    return 1.0 / (1.0 + np.exp(-v))


def split_thirds(x):
    k = x.shape[-1] // 3
    return x[..., :k], x[..., k:2 * k], x[..., 2 * k:]


def draw0():
    sh, se, t = mx_kscale(H), mx_kscale(E), mx_kscale(H)
    h = bf(np.random.standard_normal((N, H)) * 0.8)
    a = bf((1.0 + 0.1 * np.random.standard_normal(H)) * sh)
    wh_words, wh_scales = pack4(np.random.standard_normal((H, G)) / np.sqrt(H) / sh[:, None])
    p = bf(np.random.standard_normal((M, E)) * se)
    wi_words, wi_scales = pack4(np.random.standard_normal((E, G)) / np.sqrt(E) / se[:, None])
    g = bf((1.0 + 0.1 * np.random.standard_normal(H)) * t)
    wo_words, wo_scales = pack4(2.0 * np.random.standard_normal((H, W)) / np.sqrt(H) / t[:, None])
    return {
        "h": h,
        "a": a,
        "wh_words": wh_words,
        "wh_scales": wh_scales,
        "p": p,
        "wi_words": wi_words,
        "wi_scales": wi_scales,
        "g": g,
        "wo_words": wo_words,
        "wo_scales": wo_scales,
    }


def core(h, a, wh_words, wh_scales, p, wi_words, wi_scales, g, wo_words, wo_scales):
    h = f64(h)
    u = mxq(h * f64(a)[None, :], 1, "e4m3") @ unpack4(wh_words, wh_scales)
    ur, uz, un = split_thirds(u)
    v = mxq(f64(p), 1, "e4m3") @ unpack4(wi_words, wi_scales)
    vr, vz, vn = split_thirds(v)

    r = sigmoid(ur[:, None, :] + vr[None, :, :])
    z = sigmoid(uz[:, None, :] + vz[None, :, :])

    c = np.tanh(vn[None, :, :] + r * un[:, None, :])

    s = (1.0 - z) * c + z * h[:, None, :]

    sg = s * f64(g)[None, None, :]
    return mxq(sg, 2, "e4m3") @ unpack4(wo_words, wo_scales)


def setup_inputs():
    drawn = draw0()
    full = np.asarray(drawn['p']).astype(np.float64)
    scale = (np.abs(full).reshape(128, 4, 128).max(axis=(2,)) / 448.0).astype(np.float32)
    given = {}
    for key, value in drawn.items():
        if key == 'p':
            given['p_bytes'] = e4m3fn_bytes(full / np.repeat(scale.astype(np.float64), 128, axis=1))
            given['p_scale'] = scale
        else:
            given[key] = value
    return given


def reference(h, a, wh_words, wh_scales, p_bytes, p_scale, wi_words, wi_scales, g, wo_words, wo_scales):
    return core(h, a, wh_words, wh_scales, e4m3fn_values(p_bytes) * np.repeat(p_scale.astype(np.float64), 128, axis=1), wi_words, wi_scales, g, wo_words, wo_scales)

@@ -1,0 +1,321 @@
+from contextlib import ExitStack
+
+import concourse.mybir as mybir
+from concourse.masks import make_identity
+
+N, M, E, H, W = 128, 128, 512, 1024, 256
+P = 128
+NB = 4
+FLOPS = 2 * N * H * 3 * H + 2 * M * E * 3 * H + 2 * N * M * H * W
+
+F32 = mybir.dt.float32
+BF16 = mybir.dt.bfloat16
+I32 = mybir.dt.int32
+U32 = mybir.dt.uint32
+U8 = mybir.dt.uint8
+FP8 = mybir.dt.float8_e4m3fn
+FP8X4 = mybir.dt.float8_e4m3fn_x4
+FP4X4 = mybir.dt.float4_e2m1fn_x4
+ALU = mybir.AluOpType
+ACT = mybir.ActivationFunctionType
+
+
+def tile_segrnnparallelsegmentdecoder_d1p_kernel(
+    tc, h, a, wh_words, wh_scales, p_bytes, p_scale, wi_words, wi_scales, g, wo_words, wo_scales, out
+):
+    nc = tc.nc
+    with ExitStack() as ctx:
+        keep = ctx.enter_context(tc.tile_pool(name="keep", bufs=1))
+        head = ctx.enter_context(tc.tile_pool(name="head", bufs=2))
+        work = ctx.enter_context(tc.tile_pool(name="work", bufs=2))
+        vbank = ctx.enter_context(tc.psum_pool(name="vbank", bufs=1))
+        banks = ctx.enter_context(tc.psum_pool(name="banks", bufs=6))
+        ctx.enter_context(tc.manual_schedule())
+
+        h_sb = keep.tile([P, H], BF16, align_bytes=64, name="h_sb")
+        nc.sync.dma_start(out=h_sb[:], in_=h)
+        pb_sb = keep.tile([P, E], U8, align_bytes=64, name="pb_sb")
+        nc.sync.dma_start(out=pb_sb[:], in_=p_bytes)
+        ps_sb = keep.tile([P, 4], F32, name="ps_sb")
+        nc.sync.dma_start(out=ps_sb[:], in_=p_scale)
+        a_sb = keep.tile([P, 2, 4], BF16, name="a_sb")
+        nc.sync.dma_start(out=a_sb[:], in_=a.rearrange("(g p t) -> p g t", g=2, t=4))
+        g_sb = keep.tile([P, 2, 4], BF16, name="g_sb")
+        nc.sync.dma_start(out=g_sb[:], in_=g.rearrange("(g p t) -> p g t", g=2, t=4))
+
+        wh_sc = keep.tile([P, 2, 3 * H], U8, align_bytes=64, name="wh_sc")
+        wi_sc = keep.tile([P, 3 * H], U8, align_bytes=64, name="wi_sc")
+        wo_sc = keep.tile([P, 2, W], U8, align_bytes=64, name="wo_sc")
+        nc.vector.memset(wh_sc[:].bitcast(I32), 0)
+        nc.vector.memset(wi_sc[:].bitcast(I32), 0)
+        nc.vector.memset(wo_sc[:].bitcast(I32), 0)
+
+        wh_sb = [keep.tile([P, 2, 3, 1024], U8, align_bytes=64, name="wh_sb%d" % k) for k in range(2)]
+        wi_sb = [keep.tile([P, 3, 1024], U8, align_bytes=64, name="wi_sb%d" % k) for k in range(2)]
+
+        def load_words(kg):
+            for c in range(2):
+                nc.sync.dma_start(
+                    out=wh_sb[kg][:, c].bitcast(I32),
+                    in_=wh_words[c].bitcast(I32).rearrange("p (q k w) -> p q k w", q=3, k=2)[:, :, kg, :],
+                )
+            nc.sync.dma_start(
+                out=wi_sb[kg][:].bitcast(I32),
+                in_=wi_words[0].bitcast(I32).rearrange("p (q k w) -> p q k w", q=3, k=2)[:, :, kg, :],
+            )
+
+        load_words(0)
+        for q in range(4):
+            nc.sync.dma_start(
+                out=wh_sc[32 * q : 32 * q + 4].bitcast(I32),
+                in_=wh_scales[:, 4 * q : 4 * q + 4, :].rearrange("g q n -> q g n").bitcast(I32),
+            )
+        for q in range(4):
+            nc.sync.dma_start(
+                out=wi_sc[32 * q : 32 * q + 4, :].bitcast(I32),
+                in_=wi_scales[0, 4 * q : 4 * q + 4, :].bitcast(I32),
+            )
+        load_words(1)
+        wo_sb = keep.tile([P, 2, 2 * W], U8, align_bytes=64, name="wo_sb")
+        nc.sync.dma_start(out=wo_sb[:].bitcast(I32), in_=wo_words.rearrange("g p w -> p g w").bitcast(I32))
+        for q in range(4):
+            nc.sync.dma_start(
+                out=wo_sc[32 * q : 32 * q + 4].bitcast(I32),
+                in_=wo_scales[:, 4 * q : 4 * q + 4, :].rearrange("g q n -> q g n").bitcast(I32),
+            )
+
+        warm = keep.tile([P, 1], F32, name="warm")
+        nc.vector.memset(warm[:], 0.0)
+        nc.scalar.activation(out=warm[:], in_=warm[:], func=ACT.Sigmoid)
+
+        ident = keep.tile([P, P], F32, name="ident")
+        make_identity(nc, ident[:])
+
+        hT = [keep.tile([P, 4, N], F32, name="hT%d" % k) for k in range(2)]
+        hgT = [keep.tile([P, 4, N], F32, name="hgT%d" % k) for k in range(2)]
+        gF = keep.tile([P, 2, 4], F32, name="gF")
+        ha_grp = keep.tile([P, 2, N, 4], BF16, align_bytes=64, name="ha_grp")
+        ha_codes = keep.tile([P, 2, N], U32, align_bytes=64, name="ha_codes")
+        ha_sc = keep.tile([P, 2, N], U8, align_bytes=64, name="ha_sc")
+        p_codes = keep.tile([P, M], U32, align_bytes=64, name="p_codes")
+        p_sc = keep.tile([P, M], U8, align_bytes=64, name="p_sc")
+
+        pw = keep.tile([P, E], BF16, align_bytes=64, name="pw")
+        for j in range(4):
+            nc.vector.tensor_scalar(
+                out=pw[:, 128 * j : 128 * j + 128], in0=pb_sb[:, 128 * j : 128 * j + 128].bitcast(FP8),
+                scalar1=ps_sb[:, j : j + 1], scalar2=None, op0=ALU.mult,
+            )
+        h_words = h_sb[:].bitcast(F32)
+        for k in range(2):
+            xt = banks.tile([P, 2, N], F32, name="bank")
+            for u in range(2):
+                nc.tensor.transpose(xt[:, u, :], h_words[:, 256 * k + u : 256 * (k + 1) : 2], ident[:])
+            pairs = xt[:].bitcast(BF16)
+            nc.vector.tensor_tensor(
+                out=ha_grp[:, k].rearrange("p n (u e) -> p n u e", e=2),
+                in0=pairs.rearrange("p u (n e) -> p n u e", e=2),
+                in1=a_sb[:, k, :].rearrange("p (u e) -> p u e", e=2).unsqueeze(1).to_broadcast([P, N, 2, 2]),
+                op=ALU.mult,
+            )
+            nc.scalar.copy(
+                out=hT[k][:].rearrange("p (u e) n -> p u e n", e=2),
+                in_=pairs.rearrange("p u (n e) -> p u e n", e=2),
+            )
+        p_words = pw[:].bitcast(F32)
+        xt = banks.tile([P, 2, N], F32, name="bank")
+        for u in range(2):
+            nc.tensor.transpose(xt[:, u, :], p_words[:, u:256:2], ident[:])
+        p_grp = keep.tile([P, M, 4], BF16, align_bytes=64, name="p_grp")
+        nc.vector.tensor_copy(out=p_grp[:].rearrange("p m t -> p (m t)").bitcast(F32).rearrange("p (m u) -> p m u", u=2),
+                              in_=xt[:].rearrange("p u m -> p m u"))
+        nc.vector.quantize_mx(
+            out=ha_codes[:].rearrange("p k n -> p (k n)").bitcast(FP8X4),
+            scales=ha_sc[:].rearrange("p k n -> p (k n)"),
+            in_=ha_grp[:].rearrange("p k n t -> p (k n t)"),
+        )
+        nc.vector.tensor_copy(out=gF[:], in_=g_sb[:])
+        nc.vector.quantize_mx(out=p_codes[:].bitcast(FP8X4), scales=p_sc[:], in_=p_grp[:].rearrange("p m t -> p (m t)"))
+        for k in range(2):
+            nc.vector.tensor_tensor(
+                out=hgT[k][:], in0=hT[k][:], in1=gF[:, k, :].unsqueeze(2).to_broadcast([P, 4, N]), op=ALU.mult
+            )
+
+        ur = [keep.tile([P, 4, N], F32, name="ur%d" % k) for k in range(2)]
+        nuz = [keep.tile([P, 4, N], F32, name="nuz%d" % k) for k in range(2)]
+        un = [keep.tile([P, 4, N], F32, name="un%d" % k) for k in range(2)]
+        vr = [keep.tile([P, 4, M], F32, name="vr%d" % k) for k in range(2)]
+        vz = [keep.tile([P, 4, M], F32, name="vz%d" % k) for k in range(2)]
+        vn = [vbank.tile([P, 4, M], F32, name="vn%d" % k) for k in range(2)]
+
+        def project(k):
+            rows = []
+            for q in range(3):
+                acc = banks.tile([P, 512], F32, name="bank")
+                for c in range(2):
+                    nc.tensor.matmul_mx(
+                        out=acc[:], lhsT=ha_codes[:, c, :].bitcast(FP8X4), lhsT_scale=ha_sc[:, c, :],
+                        rhs=wh_sb[k][:, c, q, :].bitcast(FP4X4),
+                        rhs_scale=wh_sc[:, c, H * q + 512 * k : H * q + 512 * k + 512],
+                        start=(c == 0), stop=(c == 1),
+                    )
+                row = head.tile([P, 4, P], F32, name="urow%d" % q)
+                nc.vector.tensor_copy(out=row[:], in_=acc[:].rearrange("n (p t) -> n t p", t=4))
+                acc = banks.tile([P, 512], F32, name="bank")
+                nc.tensor.matmul_mx(
+                    out=acc[:], lhsT=p_codes[:].bitcast(FP8X4), lhsT_scale=p_sc[:],
+                    rhs=wi_sb[k][:, q, :].bitcast(FP4X4),
+                    rhs_scale=wi_sc[:, H * q + 512 * k : H * q + 512 * k + 512],
+                    start=True, stop=True,
+                )
+                row2 = head.tile([P, 4, P], F32, name="vrow%d" % q)
+                nc.scalar.copy(out=row2[:], in_=acc[:].rearrange("n (p t) -> n t p", t=4))
+                rows.append((row, row2))
+            for q in range(3):
+                row, row2 = rows[q]
+                xu = banks.tile([P, 4, N], F32, name="bank")
+                for t in range(4):
+                    nc.tensor.transpose(xu[:, t, :], row[:, t, :], ident[:])
+                if q == 1:
+                    nc.vector.tensor_scalar(out=nuz[k][:], in0=xu[:], scalar1=-1.0, scalar2=None, op0=ALU.mult)
+                else:
+                    nc.vector.tensor_copy(out=(ur[k] if q == 0 else un[k])[:], in_=xu[:])
+                if q == 2:
+                    xv = vn[k]
+                else:
+                    xv = banks.tile([P, 4, M], F32, name="bank")
+                for t in range(4):
+                    nc.tensor.transpose(xv[:, t, :], row2[:, t, :], ident[:])
+                if q < 2:
+                    nc.scalar.copy(out=(vr[k] if q == 0 else vz[k])[:], in_=xv[:])
+
+        project(0)
+        project(1)
+
+        units = 2 * (N // NB)
+        live = {}
+
+        def lanes():
+            return [(t, i) for i in range(NB) for t in range(4)]
+
+        def gate_r(j):
+            kg, n0 = j % 2, NB * (j // 2)
+            r = work.tile([P, 4, NB, M], F32, bufs=3, name="r")
+            for t, i in lanes():
+                nc.scalar.activation(out=r[:, t, i, :], in_=vr[kg][:, t, :], func=ACT.Sigmoid,
+                                     bias=ur[kg][:, t, n0 + i : n0 + i + 1])
+            live["r", j] = r
+
+        def gate_z(j):
+            kg, n0 = j % 2, NB * (j // 2)
+            z = work.tile([P, 4, NB, M], F32, bufs=3, name="z")
+            for t, i in lanes():
+                nc.scalar.activation(out=z[:, t, i, :], in_=vz[kg][:, t, :], func=ACT.Sigmoid,
+                                     bias=nuz[kg][:, t, n0 + i : n0 + i + 1], scale=-1.0)
+            live["z", j] = z
+
+        def pre_candidate(j, part):
+            kg, n0 = j % 2, NB * (j // 2)
+            if part == 0:
+                s = work.tile([P, 4, NB, M], F32, bufs=2, name="s")
+                live["s", j] = s
+            s = live["s", j]
+            r = live["r", j]
+            for t, i in lanes()[8 * part : 8 * part + 8]:
+                nc.vector.scalar_tensor_tensor(
+                    out=s[:, t, i, :], in0=r[:, t, i, :], scalar=un[kg][:, t, n0 + i : n0 + i + 1],
+                    in1=vn[kg][:, t, :], op0=ALU.mult, op1=ALU.add,
+                )
+
+        def candidate(j):
+            c = work.tile([P, 4, NB, M], F32, bufs=2, name="c")
+            nc.scalar.activation(out=c[:], in_=live["s", j][:], func=ACT.Tanh)
+            live["c", j] = c
+
+        def mix(j):
+            kg, n0 = j % 2, NB * (j // 2)
+            d = work.tile([P, 4, NB, M], F32, bufs=2, name="d")
+            c, z = live["c", j], live["z", j]
+            for t, i in lanes():
+                nc.vector.scalar_tensor_tensor(
+                    out=d[:, t, i, :], in0=c[:, t, i, :], scalar=hT[kg][:, t, n0 + i : n0 + i + 1],
+                    in1=z[:, t, i, :], op0=ALU.subtract, op1=ALU.mult,
+                )
+            live["d", j] = d
+
+        def gain(j):
+            kg, n0 = j % 2, NB * (j // 2)
+            sg = work.tile([P, 4, NB * M], BF16, bufs=2, align_bytes=64, name="sg")
+            d = live["d", j]
+            for t, i in lanes():
+                nc.vector.tensor_scalar(
+                    out=sg[:, t, M * i : M * i + M], in0=d[:, t, i, :], scalar1=gF[:, kg, t : t + 1],
+                    scalar2=hgT[kg][:, t, n0 + i : n0 + i + 1], op0=ALU.mult, op1=ALU.add,
+                )
+            live["sg", j] = sg
+
+        def interleave(j):
+            grp = work.tile([P, NB * M, 4], BF16, bufs=2, align_bytes=64, name="grp")
+            nc.vector.tensor_copy(
+                out=grp[:].rearrange("p (c i) t -> p c t i", i=4),
+                in_=live["sg", j][:].rearrange("p t (c i) -> p c t i", i=4),
+            )
+            live["grp", j] = grp
+
+        def quantize(j):
+            codes = work.tile([P, NB * M], U32, bufs=4, align_bytes=64, name="codes")
+            scales = work.tile([P, NB * M], U8, bufs=4, align_bytes=64, name="scales")
+            nc.vector.quantize_mx(
+                out=codes[:].bitcast(FP8X4), scales=scales[:], in_=live["grp", j][:].rearrange("p c t -> p (c t)")
+            )
+            live["q", j] = (codes, scales)
+
+        def project_out(b):
+            accs = []
+            for i in range(NB):
+                if i % 2 == 0:
+                    acc = banks.tile([P, 2, W], F32, name="bank")
+                    accs.append(acc)
+                for w in range(2):
+                    for kg in range(2):
+                        codes, scales = live["q", 2 * b + kg]
+                        nc.tensor.matmul_mx(
+                            out=accs[i // 2][:, i % 2, 128 * w : 128 * w + 128],
+                            lhsT=codes[:, M * i : M * i + M].bitcast(FP8X4), lhsT_scale=scales[:, M * i : M * i + M],
+                            rhs=wo_sb[:, kg, 256 * w : 256 * w + 256].bitcast(FP4X4),
+                            rhs_scale=wo_sc[:, kg, 128 * w : 128 * w + 128],
+                            start=(kg == 0), stop=(kg == 1),
+                        )
+            live["acc", b] = accs
+
+        def store(b):
+            o_sb = work.tile([P, NB, W], F32, bufs=3, name="o_sb")
+            for i, acc in enumerate(live["acc", b]):
+                nc.scalar.copy(out=o_sb[:, 2 * i : 2 * i + 2, :], in_=acc[:])
+            nc.sync.dma_start(out=out[NB * b : NB * b + NB].rearrange("n m w -> m n w"), in_=o_sb[:])
+
+        gate_r(0)
+        gate_r(1)
+        pre_candidate(0, 0)
+        pre_candidate(0, 1)
+        for j in range(units + 3):
+            if j < units:
+                candidate(j)
+                gate_z(j)
+            if j + 2 < units:
+                gate_r(j + 2)
+            if j >= 3 and j % 2 == 1:
+                store((j - 3) // 2)
+            if 1 <= j <= units:
+                mix(j - 1)
+                gain(j - 1)
+            if j + 1 < units:
+                pre_candidate(j + 1, 0)
+            if 1 <= j <= units:
+                interleave(j - 1)
+            if j + 1 < units:
+                pre_candidate(j + 1, 1)
+            if 1 <= j <= units:
+                quantize(j - 1)
+            if j >= 2 and j % 2 == 0 and j <= units:
+                project_out((j - 2) // 2)

@@ -245,7 +245,7 @@ def tile_segrnnparallelsegmentdecoder_d1p_kernel(
 
         def gain(j):
             kg, n0 = j % 2, NB * (j // 2)
-            sg = work.tile([P, 4, NB * M], BF16, bufs=2, align_bytes=64, name="sg")
+            sg = work.tile([P, 4, NB * M], BF16, bufs=3, align_bytes=64, name="sg")
             d = live["d", j]
             for t, i in lanes():
                 nc.vector.tensor_scalar(
@@ -255,10 +255,10 @@ def tile_segrnnparallelsegmentdecoder_d1p_kernel(
             live["sg", j] = sg
 
         def interleave(j):
-            grp = work.tile([P, NB * M, 4], BF16, bufs=2, align_bytes=64, name="grp")
-            nc.vector.tensor_copy(
-                out=grp[:].rearrange("p (c i) t -> p c t i", i=4),
-                in_=live["sg", j][:].rearrange("p t (c i) -> p c t i", i=4),
+            grp = work.tile([P, NB * M, 4], BF16, bufs=3, align_bytes=64, name="grp")
+            nc.gpsimd.tensor_scalar(
+                out=grp[:], in0=live["sg", j][:].rearrange("p t c -> p c t"),
+                scalar1=1.0, scalar2=0.0, op0=ALU.mult, op1=ALU.add,
             )
             live["grp", j] = grp
 
@@ -288,34 +288,37 @@ def tile_segrnnparallelsegmentdecoder_d1p_kernel(
                         )
             live["acc", b] = accs
 
-        def store(b):
-            o_sb = work.tile([P, NB, W], F32, bufs=3, name="o_sb")
-            for i, acc in enumerate(live["acc", b]):
-                nc.scalar.copy(out=o_sb[:, 2 * i : 2 * i + 2, :], in_=acc[:])
-            nc.sync.dma_start(out=out[NB * b : NB * b + NB].rearrange("n m w -> m n w"), in_=o_sb[:])
+        def empty(b, half):
+            if half == 0:
+                o_sb = work.tile([P, NB, W], F32, bufs=3, name="o_sb")
+                live["o", b] = o_sb
+            o_sb = live["o", b]
+            nc.vector.tensor_copy(out=o_sb[:, 2 * half : 2 * half + 2, :], in_=live["acc", b][half][:])
+            if half == 1:
+                nc.sync.dma_start(out=out[NB * b : NB * b + NB].rearrange("n m w -> m n w"), in_=o_sb[:])
 
         gate_r(0)
         gate_r(1)
         pre_candidate(0, 0)
         pre_candidate(0, 1)
-        for j in range(units + 3):
+        for j in range(units + 4):
             if j < units:
                 candidate(j)
                 gate_z(j)
             if j + 2 < units:
                 gate_r(j + 2)
-            if j >= 3 and j % 2 == 1:
-                store((j - 3) // 2)
             if 1 <= j <= units:
                 mix(j - 1)
-                gain(j - 1)
-            if j + 1 < units:
-                pre_candidate(j + 1, 0)
+            if 2 <= j <= units + 1:
+                quantize(j - 2)
             if 1 <= j <= units:
+                gain(j - 1)
                 interleave(j - 1)
             if j + 1 < units:
+                pre_candidate(j + 1, 0)
+            if j >= 4:
+                empty((j - 4) // 2, j % 2)
+            if j + 1 < units:
                 pre_candidate(j + 1, 1)
-            if 1 <= j <= units:
-                quantize(j - 1)
-            if j >= 2 and j % 2 == 0 and j <= units:
-                project_out((j - 2) // 2)
+            if j >= 3 and j % 2 == 1 and j <= units + 1:
+                project_out((j - 3) // 2)

@@ -26,22 +26,18 @@ def tile_segrnnparallelsegmentdecoder_d1p_kernel(
     nc = tc.nc
     with ExitStack() as ctx:
         keep = ctx.enter_context(tc.tile_pool(name="keep", bufs=1))
-        head = ctx.enter_context(tc.tile_pool(name="head", bufs=2))
+        head = ctx.enter_context(tc.tile_pool(name="head", bufs=3))
         work = ctx.enter_context(tc.tile_pool(name="work", bufs=2))
         vbank = ctx.enter_context(tc.psum_pool(name="vbank", bufs=1))
         banks = ctx.enter_context(tc.psum_pool(name="banks", bufs=6))
         ctx.enter_context(tc.manual_schedule())
 
-        h_sb = keep.tile([P, H], BF16, align_bytes=64, name="h_sb")
-        nc.sync.dma_start(out=h_sb[:], in_=h)
-        pb_sb = keep.tile([P, E], U8, align_bytes=64, name="pb_sb")
-        nc.sync.dma_start(out=pb_sb[:], in_=p_bytes)
-        ps_sb = keep.tile([P, 4], F32, name="ps_sb")
-        nc.sync.dma_start(out=ps_sb[:], in_=p_scale)
         a_sb = keep.tile([P, 2, 4], BF16, name="a_sb")
-        nc.sync.dma_start(out=a_sb[:], in_=a.rearrange("(g p t) -> p g t", g=2, t=4))
+        nc.scalar.dma_start(out=a_sb[:], in_=a.rearrange("(g p t) -> p g t", g=2, t=4))
+        ps_sb = keep.tile([P, 4], F32, name="ps_sb")
+        nc.scalar.dma_start(out=ps_sb[:], in_=p_scale)
         g_sb = keep.tile([P, 2, 4], BF16, name="g_sb")
-        nc.sync.dma_start(out=g_sb[:], in_=g.rearrange("(g p t) -> p g t", g=2, t=4))
+        nc.scalar.dma_start(out=g_sb[:], in_=g.rearrange("(g p t) -> p g t", g=2, t=4))
 
         wh_sc = keep.tile([P, 2, 3 * H], U8, align_bytes=64, name="wh_sc")
         wi_sc = keep.tile([P, 3 * H], U8, align_bytes=64, name="wi_sc")
@@ -50,21 +46,22 @@ def tile_segrnnparallelsegmentdecoder_d1p_kernel(
         nc.vector.memset(wi_sc[:].bitcast(I32), 0)
         nc.vector.memset(wo_sc[:].bitcast(I32), 0)
 
-        wh_sb = [keep.tile([P, 2, 3, 1024], U8, align_bytes=64, name="wh_sb%d" % k) for k in range(2)]
-        wi_sb = [keep.tile([P, 3, 1024], U8, align_bytes=64, name="wi_sb%d" % k) for k in range(2)]
+        wh_sb, wi_sb = {}, {}
 
-        def load_words(kg):
-            for c in range(2):
-                nc.sync.dma_start(
-                    out=wh_sb[kg][:, c].bitcast(I32),
-                    in_=wh_words[c].bitcast(I32).rearrange("p (q k w) -> p q k w", q=3, k=2)[:, :, kg, :],
-                )
+        def load_words(k, q):
+            cols = slice(512 * q + 256 * k, 512 * q + 256 * k + 256)
+            wh_sb[k, q] = keep.tile([P, 2, 1024], U8, align_bytes=64, name="wh_sb%d%d" % (k, q))
             nc.sync.dma_start(
-                out=wi_sb[kg][:].bitcast(I32),
-                in_=wi_words[0].bitcast(I32).rearrange("p (q k w) -> p q k w", q=3, k=2)[:, :, kg, :],
+                out=wh_sb[k, q][:].bitcast(I32), in_=wh_words.bitcast(I32)[:, :, cols].rearrange("g p w -> p g w")
             )
+            wi_sb[k, q] = keep.tile([P, 1024], U8, align_bytes=64, name="wi_sb%d%d" % (k, q))
+            nc.sync.dma_start(out=wi_sb[k, q][:].bitcast(I32), in_=wi_words[0].bitcast(I32)[:, cols])
 
-        load_words(0)
+        h_sb = keep.tile([P, H], BF16, align_bytes=64, name="h_sb")
+        nc.sync.dma_start(out=h_sb[:], in_=h)
+        pb_sb = keep.tile([P, E], U8, align_bytes=64, name="pb_sb")
+        nc.sync.dma_start(out=pb_sb[:], in_=p_bytes)
+        load_words(0, 0)
         for q in range(4):
             nc.sync.dma_start(
                 out=wh_sc[32 * q : 32 * q + 4].bitcast(I32),
@@ -75,7 +72,10 @@ def tile_segrnnparallelsegmentdecoder_d1p_kernel(
                 out=wi_sc[32 * q : 32 * q + 4, :].bitcast(I32),
                 in_=wi_scales[0, 4 * q : 4 * q + 4, :].bitcast(I32),
             )
-        load_words(1)
+        load_words(0, 1)
+        load_words(0, 2)
+        for q in range(3):
+            load_words(1, q)
         wo_sb = keep.tile([P, 2, 2 * W], U8, align_bytes=64, name="wo_sb")
         nc.sync.dma_start(out=wo_sb[:].bitcast(I32), in_=wo_words.rearrange("g p w -> p g w").bitcast(I32))
         for q in range(4):
@@ -148,49 +148,47 @@ def tile_segrnnparallelsegmentdecoder_d1p_kernel(
         vz = [keep.tile([P, 4, M], F32, name="vz%d" % k) for k in range(2)]
         vn = [vbank.tile([P, 4, M], F32, name="vn%d" % k) for k in range(2)]
 
-        def project(k):
-            rows = []
-            for q in range(3):
-                acc = banks.tile([P, 512], F32, name="bank")
-                for c in range(2):
-                    nc.tensor.matmul_mx(
-                        out=acc[:], lhsT=ha_codes[:, c, :].bitcast(FP8X4), lhsT_scale=ha_sc[:, c, :],
-                        rhs=wh_sb[k][:, c, q, :].bitcast(FP4X4),
-                        rhs_scale=wh_sc[:, c, H * q + 512 * k : H * q + 512 * k + 512],
-                        start=(c == 0), stop=(c == 1),
-                    )
-                row = head.tile([P, 4, P], F32, name="urow%d" % q)
-                nc.vector.tensor_copy(out=row[:], in_=acc[:].rearrange("n (p t) -> n t p", t=4))
-                acc = banks.tile([P, 512], F32, name="bank")
-                nc.tensor.matmul_mx(
-                    out=acc[:], lhsT=p_codes[:].bitcast(FP8X4), lhsT_scale=p_sc[:],
-                    rhs=wi_sb[k][:, q, :].bitcast(FP4X4),
-                    rhs_scale=wi_sc[:, H * q + 512 * k : H * q + 512 * k + 512],
-                    start=True, stop=True,
-                )
-                row2 = head.tile([P, 4, P], F32, name="vrow%d" % q)
-                nc.scalar.copy(out=row2[:], in_=acc[:].rearrange("n (p t) -> n t p", t=4))
-                rows.append((row, row2))
-            for q in range(3):
-                row, row2 = rows[q]
-                xu = banks.tile([P, 4, N], F32, name="bank")
-                for t in range(4):
-                    nc.tensor.transpose(xu[:, t, :], row[:, t, :], ident[:])
-                if q == 1:
-                    nc.vector.tensor_scalar(out=nuz[k][:], in0=xu[:], scalar1=-1.0, scalar2=None, op0=ALU.mult)
-                else:
-                    nc.vector.tensor_copy(out=(ur[k] if q == 0 else un[k])[:], in_=xu[:])
-                if q == 2:
-                    xv = vn[k]
-                else:
-                    xv = banks.tile([P, 4, M], F32, name="bank")
-                for t in range(4):
-                    nc.tensor.transpose(xv[:, t, :], row2[:, t, :], ident[:])
-                if q < 2:
-                    nc.scalar.copy(out=(vr[k] if q == 0 else vz[k])[:], in_=xv[:])
+        rows = {}
 
-        project(0)
-        project(1)
+        def multiply(k, q):
+            acc = banks.tile([P, 512], F32, name="bank")
+            for c in range(2):
+                nc.tensor.matmul_mx(
+                    out=acc[:], lhsT=ha_codes[:, c, :].bitcast(FP8X4), lhsT_scale=ha_sc[:, c, :],
+                    rhs=wh_sb[k, q][:, c, :].bitcast(FP4X4),
+                    rhs_scale=wh_sc[:, c, H * q + 512 * k : H * q + 512 * k + 512],
+                    start=(c == 0), stop=(c == 1),
+                )
+            u_row = head.tile([P, 4, P], F32, name="u_row")
+            nc.vector.tensor_copy(out=u_row[:], in_=acc[:].rearrange("n (p t) -> n t p", t=4))
+            acc = banks.tile([P, 512], F32, name="bank")
+            nc.tensor.matmul_mx(
+                out=acc[:], lhsT=p_codes[:].bitcast(FP8X4), lhsT_scale=p_sc[:],
+                rhs=wi_sb[k, q][:].bitcast(FP4X4),
+                rhs_scale=wi_sc[:, H * q + 512 * k : H * q + 512 * k + 512],
+                start=True, stop=True,
+            )
+            v_row = head.tile([P, 4, P], F32, name="v_row")
+            nc.scalar.copy(out=v_row[:], in_=acc[:].rearrange("n (p t) -> n t p", t=4))
+            rows[k, q] = (u_row, v_row)
+
+        def turn(k, q):
+            u_row, v_row = rows[k, q]
+            xu = banks.tile([P, 4, N], F32, name="bank")
+            for t in range(4):
+                nc.tensor.transpose(xu[:, t, :], u_row[:, t, :], ident[:])
+            if q == 1:
+                nc.vector.tensor_scalar(out=nuz[k][:], in0=xu[:], scalar1=-1.0, scalar2=None, op0=ALU.mult)
+            else:
+                nc.vector.tensor_copy(out=(ur[k] if q == 0 else un[k])[:], in_=xu[:])
+            if q == 2:
+                xv = vn[k]
+            else:
+                xv = banks.tile([P, 4, M], F32, name="bank")
+            for t in range(4):
+                nc.tensor.transpose(xv[:, t, :], v_row[:, t, :], ident[:])
+            if q < 2:
+                nc.scalar.copy(out=(vr[k] if q == 0 else vz[k])[:], in_=xv[:])
 
         units = 2 * (N // NB)
         live = {}
@@ -217,7 +215,7 @@ def tile_segrnnparallelsegmentdecoder_d1p_kernel(
         def pre_candidate(j, part):
             kg, n0 = j % 2, NB * (j // 2)
             if part == 0:
-                s = work.tile([P, 4, NB, M], F32, bufs=2, name="s")
+                s = work.tile([P, 4, NB, M], F32, bufs=3, name="s")
                 live["s", j] = s
             s = live["s", j]
             r = live["r", j]
@@ -227,98 +225,153 @@ def tile_segrnnparallelsegmentdecoder_d1p_kernel(
                     in1=vn[kg][:, t, :], op0=ALU.mult, op1=ALU.add,
                 )
 
-        def candidate(j):
-            c = work.tile([P, 4, NB, M], F32, bufs=2, name="c")
-            nc.scalar.activation(out=c[:], in_=live["s", j][:], func=ACT.Tanh)
-            live["c", j] = c
+        def candidate(j, cut):
+            if cut.start == 0:
+                c = work.tile([P, 4, NB, M], F32, bufs=2, name="c")
+                live["c", j] = c
+            nc.scalar.activation(out=live["c", j][:, :, cut, :], in_=live["s", j][:, :, cut, :], func=ACT.Tanh)
 
-        def mix(j):
+        def mix(j, cut):
             kg, n0 = j % 2, NB * (j // 2)
-            d = work.tile([P, 4, NB, M], F32, bufs=2, name="d")
-            c, z = live["c", j], live["z", j]
-            for t, i in lanes():
-                nc.vector.scalar_tensor_tensor(
-                    out=d[:, t, i, :], in0=c[:, t, i, :], scalar=hT[kg][:, t, n0 + i : n0 + i + 1],
-                    in1=z[:, t, i, :], op0=ALU.subtract, op1=ALU.mult,
-                )
-            live["d", j] = d
+            if cut.start == 0:
+                d = work.tile([P, 4, NB, M], F32, bufs=2, name="d")
+                live["d", j] = d
+            d, c, z = live["d", j], live["c", j], live["z", j]
+            for i in range(cut.start, cut.stop):
+                for t in range(4):
+                    nc.vector.scalar_tensor_tensor(
+                        out=d[:, t, i, :], in0=c[:, t, i, :], scalar=hT[kg][:, t, n0 + i : n0 + i + 1],
+                        in1=z[:, t, i, :], op0=ALU.subtract, op1=ALU.mult,
+                    )
 
-        def gain(j):
+        def gain(j, cut):
             kg, n0 = j % 2, NB * (j // 2)
-            sg = work.tile([P, 4, NB * M], BF16, bufs=3, align_bytes=64, name="sg")
-            d = live["d", j]
-            for t, i in lanes():
-                nc.vector.tensor_scalar(
-                    out=sg[:, t, M * i : M * i + M], in0=d[:, t, i, :], scalar1=gF[:, kg, t : t + 1],
-                    scalar2=hgT[kg][:, t, n0 + i : n0 + i + 1], op0=ALU.mult, op1=ALU.add,
+            if cut.start == 0:
+                sg = work.tile([P, 4, NB * M], BF16, bufs=3, align_bytes=64, name="sg")
+                live["sg", j] = sg
+            sg, d = live["sg", j], live["d", j]
+            for i in range(cut.start, cut.stop):
+                for t in range(4):
+                    nc.vector.tensor_scalar(
+                        out=sg[:, t, M * i : M * i + M], in0=d[:, t, i, :], scalar1=gF[:, kg, t : t + 1],
+                        scalar2=hgT[kg][:, t, n0 + i : n0 + i + 1], op0=ALU.mult, op1=ALU.add,
+                    )
+
+        def interleave(j, cut):
+            if cut.start == 0:
+                grp = work.tile([P, NB * M, 4], BF16, bufs=3, align_bytes=64, name="grp")
+                live["grp", j] = grp
+            cols = slice(M * cut.start, M * cut.stop)
+            dst, src = live["grp", j][:, cols, :], live["sg", j][:, :, cols]
+            if j >= units - 2:
+                nc.vector.tensor_copy(
+                    out=dst.rearrange("p (c i) t -> p c t i", i=4), in_=src.rearrange("p t (c i) -> p c t i", i=4)
                 )
-            live["sg", j] = sg
+            else:
+                nc.gpsimd.tensor_scalar(
+                    out=dst, in0=src.rearrange("p t c -> p c t"), scalar1=1.0, scalar2=0.0, op0=ALU.mult, op1=ALU.add
+                )
 
-        def interleave(j):
-            grp = work.tile([P, NB * M, 4], BF16, bufs=3, align_bytes=64, name="grp")
-            nc.gpsimd.tensor_scalar(
-                out=grp[:], in0=live["sg", j][:].rearrange("p t c -> p c t"),
-                scalar1=1.0, scalar2=0.0, op0=ALU.mult, op1=ALU.add,
-            )
-            live["grp", j] = grp
-
-        def quantize(j):
-            codes = work.tile([P, NB * M], U32, bufs=4, align_bytes=64, name="codes")
-            scales = work.tile([P, NB * M], U8, bufs=4, align_bytes=64, name="scales")
+        def quantize(j, cut):
+            if cut.start == 0:
+                codes = work.tile([P, NB * M], U32, bufs=4, align_bytes=64, name="codes")
+                scales = work.tile([P, NB * M], U8, bufs=4, align_bytes=64, name="scales")
+                live["q", j] = (codes, scales)
+            codes, scales = live["q", j]
+            cols = slice(M * cut.start, M * cut.stop)
             nc.vector.quantize_mx(
-                out=codes[:].bitcast(FP8X4), scales=scales[:], in_=live["grp", j][:].rearrange("p c t -> p (c t)")
+                out=codes[:, cols].bitcast(FP8X4), scales=scales[:, cols],
+                in_=live["grp", j][:, cols, :].rearrange("p c t -> p (c t)"),
             )
-            live["q", j] = (codes, scales)
 
-        def project_out(b):
-            accs = []
-            for i in range(NB):
-                if i % 2 == 0:
-                    acc = banks.tile([P, 2, W], F32, name="bank")
-                    accs.append(acc)
-                for w in range(2):
-                    for kg in range(2):
-                        codes, scales = live["q", 2 * b + kg]
-                        nc.tensor.matmul_mx(
-                            out=accs[i // 2][:, i % 2, 128 * w : 128 * w + 128],
-                            lhsT=codes[:, M * i : M * i + M].bitcast(FP8X4), lhsT_scale=scales[:, M * i : M * i + M],
-                            rhs=wo_sb[:, kg, 256 * w : 256 * w + 256].bitcast(FP4X4),
-                            rhs_scale=wo_sc[:, kg, 128 * w : 128 * w + 128],
-                            start=(kg == 0), stop=(kg == 1),
-                        )
-            live["acc", b] = accs
+        def project_out(b, cut):
+            for half in range(cut.start // 2, cut.stop // 2):
+                acc = banks.tile([P, 2, W], F32, name="bank")
+                for i in range(2):
+                    rows_n = slice(M * (2 * half + i), M * (2 * half + i) + M)
+                    for w in range(2):
+                        for kg in range(2):
+                            codes, scales = live["q", 2 * b + kg]
+                            nc.tensor.matmul_mx(
+                                out=acc[:, i, 128 * w : 128 * w + 128],
+                                lhsT=codes[:, rows_n].bitcast(FP8X4), lhsT_scale=scales[:, rows_n],
+                                rhs=wo_sb[:, kg, 256 * w : 256 * w + 256].bitcast(FP4X4),
+                                rhs_scale=wo_sc[:, kg, 128 * w : 128 * w + 128],
+                                start=(kg == 0), stop=(kg == 1),
+                            )
+                live["acc", b, half] = acc
 
         def empty(b, half):
             if half == 0:
                 o_sb = work.tile([P, NB, W], F32, bufs=3, name="o_sb")
                 live["o", b] = o_sb
-            o_sb = live["o", b]
-            nc.vector.tensor_copy(out=o_sb[:, 2 * half : 2 * half + 2, :], in_=live["acc", b][half][:])
+            part = slice(2 * half, 2 * half + 2)
+            nc.vector.tensor_copy(out=live["o", b][:, part, :], in_=live["acc", b, half][:])
             if half == 1:
-                nc.sync.dma_start(out=out[NB * b : NB * b + NB].rearrange("n m w -> m n w"), in_=o_sb[:])
+                nc.sync.dma_start(out=out[NB * b : NB * b + NB].rearrange("n m w -> m n w"), in_=live["o", b][:])
 
+        whole, halves = [slice(0, NB)], [slice(0, 2), slice(2, NB)]
+
+        multiply(0, 0)
+        turn(0, 0)
         gate_r(0)
-        gate_r(1)
+        multiply(0, 1)
+        multiply(0, 2)
+        turn(0, 1)
+        turn(0, 2)
         pre_candidate(0, 0)
         pre_candidate(0, 1)
-        for j in range(units + 4):
-            if j < units:
-                candidate(j)
-                gate_z(j)
+        gate_z(0)
+        candidate(0, whole[0])
+        multiply(1, 0)
+        turn(1, 0)
+        gate_r(1)
+        multiply(1, 1)
+        multiply(1, 2)
+        turn(1, 1)
+        turn(1, 2)
+        pre_candidate(1, 0)
+        pre_candidate(1, 1)
+        gate_r(2)
+        for j in range(1, units):
+            gate_z(j)
+            for cut in whole if j < units - 1 else halves:
+                candidate(j, cut)
             if j + 2 < units:
                 gate_r(j + 2)
-            if 1 <= j <= units:
-                mix(j - 1)
-            if 2 <= j <= units + 1:
-                quantize(j - 2)
-            if 1 <= j <= units:
-                gain(j - 1)
-                interleave(j - 1)
+            mix(j - 1, whole[0])
+            if j >= 2:
+                quantize(j - 2, whole[0])
+            gain(j - 1, whole[0])
+            interleave(j - 1, whole[0])
             if j + 1 < units:
                 pre_candidate(j + 1, 0)
             if j >= 4:
                 empty((j - 4) // 2, j % 2)
             if j + 1 < units:
                 pre_candidate(j + 1, 1)
-            if j >= 3 and j % 2 == 1 and j <= units + 1:
-                project_out((j - 3) // 2)
+            if j >= 3 and j % 2 == 1:
+                project_out((j - 3) // 2, whole[0])
+
+        last, b = units - 1, N // NB - 1
+        o_sb = work.tile([P, NB, W], F32, bufs=3, name="o_sb")
+        mix(last, halves[0])
+        quantize(last - 1, whole[0])
+        gain(last, halves[0])
+        mix(last, halves[1])
+        interleave(last, halves[0])
+        empty(b - 1, 0)
+        quantize(last, halves[0])
+        project_out(b, halves[0])
+        gain(last, halves[1])
+        empty(b - 1, 1)
+        interleave(last, halves[1])
+        quantize(last, halves[1])
+        project_out(b, halves[1])
+        for half in range(2):
+            part = slice(2 * half, 2 * half + 2)
+            copy_out = nc.scalar.copy if half == 0 else nc.vector.tensor_copy
+            copy_out(out=o_sb[:, part, :], in_=live["acc", b, half][:])
+            nc.sync.dma_start(
+                out=out[NB * b + 2 * half : NB * b + 2 * half + 2].rearrange("n m w -> m n w"), in_=o_sb[:, part, :]
+            )

@@ -29,7 +29,8 @@ def tile_segrnnparallelsegmentdecoder_d1p_kernel(
         head = ctx.enter_context(tc.tile_pool(name="head", bufs=3))
         work = ctx.enter_context(tc.tile_pool(name="work", bufs=2))
         vbank = ctx.enter_context(tc.psum_pool(name="vbank", bufs=1))
-        banks = ctx.enter_context(tc.psum_pool(name="banks", bufs=6))
+        banks = ctx.enter_context(tc.psum_pool(name="banks", bufs=4))
+        out_banks = ctx.enter_context(tc.psum_pool(name="out_banks", bufs=2))
         ctx.enter_context(tc.manual_schedule())
 
         a_sb = keep.tile([P, 2, 4], BF16, name="a_sb")
@@ -61,7 +62,7 @@ def tile_segrnnparallelsegmentdecoder_d1p_kernel(
         nc.sync.dma_start(out=h_sb[:], in_=h)
         pb_sb = keep.tile([P, E], U8, align_bytes=64, name="pb_sb")
         nc.sync.dma_start(out=pb_sb[:], in_=p_bytes)
-        load_words(0, 0)
+        load_words(0, 1)
         for q in range(4):
             nc.sync.dma_start(
                 out=wh_sc[32 * q : 32 * q + 4].bitcast(I32),
@@ -72,10 +73,8 @@ def tile_segrnnparallelsegmentdecoder_d1p_kernel(
                 out=wi_sc[32 * q : 32 * q + 4, :].bitcast(I32),
                 in_=wi_scales[0, 4 * q : 4 * q + 4, :].bitcast(I32),
             )
-        load_words(0, 1)
-        load_words(0, 2)
-        for q in range(3):
-            load_words(1, q)
+        for k, q in ((0, 0), (0, 2), (1, 1), (1, 0), (1, 2)):
+            load_words(k, q)
         wo_sb = keep.tile([P, 2, 2 * W], U8, align_bytes=64, name="wo_sb")
         nc.sync.dma_start(out=wo_sb[:].bitcast(I32), in_=wo_words.rearrange("g p w -> p g w").bitcast(I32))
         for q in range(4):
@@ -142,10 +141,10 @@ def tile_segrnnparallelsegmentdecoder_d1p_kernel(
             )
 
         ur = [keep.tile([P, 4, N], F32, name="ur%d" % k) for k in range(2)]
-        nuz = [keep.tile([P, 4, N], F32, name="nuz%d" % k) for k in range(2)]
         un = [keep.tile([P, 4, N], F32, name="un%d" % k) for k in range(2)]
         vr = [keep.tile([P, 4, M], F32, name="vr%d" % k) for k in range(2)]
-        vz = [keep.tile([P, 4, M], F32, name="vz%d" % k) for k in range(2)]
+        vz_row = {}
+        park = out[N - NB : N].rearrange("n m w -> (n m w)").rearrange("(k n c) -> k n c", k=2, c=512)
         vn = [vbank.tile([P, 4, M], F32, name="vn%d" % k) for k in range(2)]
 
         rows = {}
@@ -168,7 +167,12 @@ def tile_segrnnparallelsegmentdecoder_d1p_kernel(
                 rhs_scale=wi_sc[:, H * q + 512 * k : H * q + 512 * k + 512],
                 start=True, stop=True,
             )
-            v_row = head.tile([P, 4, P], F32, name="v_row")
+            if q == 1:
+                nc.sync.dma_start(out=park[k], in_=u_row[:].rearrange("n t p -> n (t p)"))
+                v_row = keep.tile([P, 4, P], F32, name="vz_row%d" % k)
+                vz_row[k] = v_row
+            else:
+                v_row = head.tile([P, 4, P], F32, name="v_row")
             nc.scalar.copy(out=v_row[:], in_=acc[:].rearrange("n (p t) -> n t p", t=4))
             rows[k, q] = (u_row, v_row)
 
@@ -177,18 +181,12 @@ def tile_segrnnparallelsegmentdecoder_d1p_kernel(
             xu = banks.tile([P, 4, N], F32, name="bank")
             for t in range(4):
                 nc.tensor.transpose(xu[:, t, :], u_row[:, t, :], ident[:])
-            if q == 1:
-                nc.vector.tensor_scalar(out=nuz[k][:], in0=xu[:], scalar1=-1.0, scalar2=None, op0=ALU.mult)
-            else:
-                nc.vector.tensor_copy(out=(ur[k] if q == 0 else un[k])[:], in_=xu[:])
-            if q == 2:
-                xv = vn[k]
-            else:
-                xv = banks.tile([P, 4, M], F32, name="bank")
+            nc.vector.tensor_copy(out=(ur[k] if q == 0 else un[k])[:], in_=xu[:])
+            xv = vn[k] if q == 2 else banks.tile([P, 4, M], F32, name="bank")
             for t in range(4):
                 nc.tensor.transpose(xv[:, t, :], v_row[:, t, :], ident[:])
-            if q < 2:
-                nc.scalar.copy(out=(vr[k] if q == 0 else vz[k])[:], in_=xv[:])
+            if q == 0:
+                nc.scalar.copy(out=vr[k][:], in_=xv[:])
 
         units = 2 * (N // NB)
         live = {}
@@ -204,18 +202,37 @@ def tile_segrnnparallelsegmentdecoder_d1p_kernel(
                                      bias=ur[kg][:, t, n0 + i : n0 + i + 1])
             live["r", j] = r
 
-        def gate_z(j):
+        def spread(j):
             kg, n0 = j % 2, NB * (j // 2)
+            uz = work.tile([P, NB, 4, P], F32, bufs=3, name="uz")
+            nc.sync.dma_start(
+                out=uz[:].rearrange("m i t p -> m (i t p)"),
+                in_=park[kg, n0 : n0 + NB, :].rearrange("n c -> (n c)").partition_broadcast(P),
+            )
+            live["uz", j] = uz
+
+        def sum_z(j):
+            kg = j % 2
+            uz = live["uz", j]
+            sums = []
+            for i in range(NB):
+                bank = banks.tile([P, 4, M], F32, name="bank")
+                for t in range(4):
+                    nc.tensor.matmul(bank[:, t, :], lhsT=vz_row[kg][:, t, :], rhs=ident[:], start=True, stop=False, is_transpose=True)
+                    nc.tensor.matmul(bank[:, t, :], lhsT=uz[:, i, t, :], rhs=ident[:], start=False, stop=True, is_transpose=True)
+                sums.append(bank)
+            live["xz", j] = sums
+
+        def gate_z(j):
             z = work.tile([P, 4, NB, M], F32, bufs=3, name="z")
-            for t, i in lanes():
-                nc.scalar.activation(out=z[:, t, i, :], in_=vz[kg][:, t, :], func=ACT.Sigmoid,
-                                     bias=nuz[kg][:, t, n0 + i : n0 + i + 1], scale=-1.0)
+            for i in range(NB):
+                nc.scalar.activation(out=z[:, :, i, :], in_=live["xz", j][i][:], func=ACT.Sigmoid, scale=-1.0)
             live["z", j] = z
 
         def pre_candidate(j, part):
             kg, n0 = j % 2, NB * (j // 2)
             if part == 0:
-                s = work.tile([P, 4, NB, M], F32, bufs=3, name="s")
+                s = work.tile([P, 4, NB, M], F32, bufs=2, name="s")
                 live["s", j] = s
             s = live["s", j]
             r = live["r", j]
@@ -247,7 +264,7 @@ def tile_segrnnparallelsegmentdecoder_d1p_kernel(
         def gain(j, cut):
             kg, n0 = j % 2, NB * (j // 2)
             if cut.start == 0:
-                sg = work.tile([P, 4, NB * M], BF16, bufs=3, align_bytes=64, name="sg")
+                sg = work.tile([P, 4, NB * M], BF16, bufs=2, align_bytes=64, name="sg")
                 live["sg", j] = sg
             sg, d = live["sg", j], live["d", j]
             for i in range(cut.start, cut.stop):
@@ -259,7 +276,7 @@ def tile_segrnnparallelsegmentdecoder_d1p_kernel(
 
         def interleave(j, cut):
             if cut.start == 0:
-                grp = work.tile([P, NB * M, 4], BF16, bufs=3, align_bytes=64, name="grp")
+                grp = work.tile([P, NB * M, 4], BF16, bufs=2, align_bytes=64, name="grp")
                 live["grp", j] = grp
             cols = slice(M * cut.start, M * cut.stop)
             dst, src = live["grp", j][:, cols, :], live["sg", j][:, :, cols]
@@ -286,7 +303,7 @@ def tile_segrnnparallelsegmentdecoder_d1p_kernel(
 
         def project_out(b, cut):
             for half in range(cut.start // 2, cut.stop // 2):
-                acc = banks.tile([P, 2, W], F32, name="bank")
+                acc = out_banks.tile([P, 2, W], F32, name="acc")
                 for i in range(2):
                     rows_n = slice(M * (2 * half + i), M * (2 * half + i) + M)
                     for w in range(2):
@@ -312,26 +329,29 @@ def tile_segrnnparallelsegmentdecoder_d1p_kernel(
 
         whole, halves = [slice(0, NB)], [slice(0, 2), slice(2, NB)]
 
+        multiply(0, 1)
+        spread(0)
         multiply(0, 0)
         turn(0, 0)
         gate_r(0)
-        multiply(0, 1)
         multiply(0, 2)
-        turn(0, 1)
         turn(0, 2)
+        multiply(1, 1)
+        spread(1)
         pre_candidate(0, 0)
         pre_candidate(0, 1)
-        gate_z(0)
-        candidate(0, whole[0])
         multiply(1, 0)
         turn(1, 0)
         gate_r(1)
-        multiply(1, 1)
+        candidate(0, whole[0])
         multiply(1, 2)
-        turn(1, 1)
         turn(1, 2)
+        sum_z(0)
+        gate_z(0)
         pre_candidate(1, 0)
         pre_candidate(1, 1)
+        spread(2)
+        sum_z(1)
         gate_r(2)
         for j in range(1, units):
             gate_z(j)
@@ -339,6 +359,9 @@ def tile_segrnnparallelsegmentdecoder_d1p_kernel(
                 candidate(j, cut)
             if j + 2 < units:
                 gate_r(j + 2)
+                spread(j + 2)
+            if j + 1 < units:
+                sum_z(j + 1)
             mix(j - 1, whole[0])
             if j >= 2:
                 quantize(j - 2, whole[0])
@@ -350,17 +373,18 @@ def tile_segrnnparallelsegmentdecoder_d1p_kernel(
                 empty((j - 4) // 2, j % 2)
             if j + 1 < units:
                 pre_candidate(j + 1, 1)
-            if j >= 3 and j % 2 == 1:
-                project_out((j - 3) // 2, whole[0])
+            if j >= 3:
+                project_out((j - 3) // 2, halves[(j - 3) % 2])
 
         last, b = units - 1, N // NB - 1
         o_sb = work.tile([P, NB, W], F32, bufs=3, name="o_sb")
         mix(last, halves[0])
         quantize(last - 1, whole[0])
+        empty(b - 1, 0)
+        project_out(b - 1, halves[1])
         gain(last, halves[0])
         mix(last, halves[1])
         interleave(last, halves[0])
-        empty(b - 1, 0)
         quantize(last, halves[0])
         project_out(b, halves[0])
         gain(last, halves[1])

@@ -5,7 +5,11 @@ from concourse.masks import make_identity
 
 N, M, E, H, W = 128, 128, 512, 1024, 256
 P = 128
+T = 4
+HALF = P * T
+R_GATE, Z_GATE, N_GATE = 0, 1, 2
 NB = 4
+UNITS = 2 * N // NB
 FLOPS = 2 * N * H * 3 * H + 2 * M * E * 3 * H + 2 * N * M * H * W
 
 F32 = mybir.dt.float32
@@ -28,41 +32,40 @@ def tile_segrnnparallelsegmentdecoder_d1p_kernel(
         keep = ctx.enter_context(tc.tile_pool(name="keep", bufs=1))
         head = ctx.enter_context(tc.tile_pool(name="head", bufs=3))
         work = ctx.enter_context(tc.tile_pool(name="work", bufs=2))
-        vbank = ctx.enter_context(tc.psum_pool(name="vbank", bufs=1))
+        vn_banks = ctx.enter_context(tc.psum_pool(name="vn_banks", bufs=1))
         banks = ctx.enter_context(tc.psum_pool(name="banks", bufs=4))
         out_banks = ctx.enter_context(tc.psum_pool(name="out_banks", bufs=2))
         ctx.enter_context(tc.manual_schedule())
 
-        a_sb = keep.tile([P, 2, 4], BF16, name="a_sb")
-        nc.scalar.dma_start(out=a_sb[:], in_=a.rearrange("(g p t) -> p g t", g=2, t=4))
-        ps_sb = keep.tile([P, 4], F32, name="ps_sb")
-        nc.scalar.dma_start(out=ps_sb[:], in_=p_scale)
-        g_sb = keep.tile([P, 2, 4], BF16, name="g_sb")
-        nc.scalar.dma_start(out=g_sb[:], in_=g.rearrange("(g p t) -> p g t", g=2, t=4))
+        a_sb = keep.tile([P, 2, T], BF16, name="a_sb")
+        nc.scalar.dma_start(out=a_sb[:], in_=a.rearrange("(g p t) -> p g t", g=2, t=T))
+        p_scale_sb = keep.tile([P, E // 128], F32, name="p_scale_sb")
+        nc.scalar.dma_start(out=p_scale_sb[:], in_=p_scale)
+        g_sb = keep.tile([P, 2, T], BF16, name="g_sb")
+        nc.scalar.dma_start(out=g_sb[:], in_=g.rearrange("(g p t) -> p g t", g=2, t=T))
 
         wh_sc = keep.tile([P, 2, 3 * H], U8, align_bytes=64, name="wh_sc")
         wi_sc = keep.tile([P, 3 * H], U8, align_bytes=64, name="wi_sc")
         wo_sc = keep.tile([P, 2, W], U8, align_bytes=64, name="wo_sc")
-        nc.vector.memset(wh_sc[:].bitcast(I32), 0)
-        nc.vector.memset(wi_sc[:].bitcast(I32), 0)
-        nc.vector.memset(wo_sc[:].bitcast(I32), 0)
+        for plane in (wh_sc, wi_sc, wo_sc):
+            nc.vector.memset(plane[:].bitcast(I32), 0)
 
         wh_sb, wi_sb = {}, {}
 
         def load_words(k, q):
-            cols = slice(512 * q + 256 * k, 512 * q + 256 * k + 256)
-            wh_sb[k, q] = keep.tile([P, 2, 1024], U8, align_bytes=64, name="wh_sb%d%d" % (k, q))
+            cols = slice((q * H + k * HALF) // 2, (q * H + (k + 1) * HALF) // 2)
+            wh_sb[k, q] = keep.tile([P, 2, 2 * HALF], U8, align_bytes=64, name="wh_sb%d%d" % (k, q))
             nc.sync.dma_start(
                 out=wh_sb[k, q][:].bitcast(I32), in_=wh_words.bitcast(I32)[:, :, cols].rearrange("g p w -> p g w")
             )
-            wi_sb[k, q] = keep.tile([P, 1024], U8, align_bytes=64, name="wi_sb%d%d" % (k, q))
+            wi_sb[k, q] = keep.tile([P, 2 * HALF], U8, align_bytes=64, name="wi_sb%d%d" % (k, q))
             nc.sync.dma_start(out=wi_sb[k, q][:].bitcast(I32), in_=wi_words[0].bitcast(I32)[:, cols])
 
         h_sb = keep.tile([P, H], BF16, align_bytes=64, name="h_sb")
         nc.sync.dma_start(out=h_sb[:], in_=h)
-        pb_sb = keep.tile([P, E], U8, align_bytes=64, name="pb_sb")
-        nc.sync.dma_start(out=pb_sb[:], in_=p_bytes)
-        load_words(0, 1)
+        p_bytes_sb = keep.tile([P, E], U8, align_bytes=64, name="p_bytes_sb")
+        nc.sync.dma_start(out=p_bytes_sb[:], in_=p_bytes)
+        load_words(0, R_GATE)
         for q in range(4):
             nc.sync.dma_start(
                 out=wh_sc[32 * q : 32 * q + 4].bitcast(I32),
@@ -70,10 +73,9 @@ def tile_segrnnparallelsegmentdecoder_d1p_kernel(
             )
         for q in range(4):
             nc.sync.dma_start(
-                out=wi_sc[32 * q : 32 * q + 4, :].bitcast(I32),
-                in_=wi_scales[0, 4 * q : 4 * q + 4, :].bitcast(I32),
+                out=wi_sc[32 * q : 32 * q + 4, :].bitcast(I32), in_=wi_scales[0, 4 * q : 4 * q + 4, :].bitcast(I32)
             )
-        for k, q in ((0, 0), (0, 2), (1, 1), (1, 0), (1, 2)):
+        for k, q in ((0, Z_GATE), (0, N_GATE), (1, R_GATE), (1, Z_GATE), (1, N_GATE)):
             load_words(k, q)
         wo_sb = keep.tile([P, 2, 2 * W], U8, align_bytes=64, name="wo_sb")
         nc.sync.dma_start(out=wo_sb[:].bitcast(I32), in_=wo_words.rearrange("g p w -> p g w").bitcast(I32))
@@ -90,29 +92,35 @@ def tile_segrnnparallelsegmentdecoder_d1p_kernel(
         ident = keep.tile([P, P], F32, name="ident")
         make_identity(nc, ident[:])
 
-        hT = [keep.tile([P, 4, N], F32, name="hT%d" % k) for k in range(2)]
-        hgT = [keep.tile([P, 4, N], F32, name="hgT%d" % k) for k in range(2)]
-        gF = keep.tile([P, 2, 4], F32, name="gF")
-        ha_grp = keep.tile([P, 2, N, 4], BF16, align_bytes=64, name="ha_grp")
+        hT = [keep.tile([P, T, N], F32, name="hT%d" % k) for k in range(2)]
+        hgT = [keep.tile([P, T, N], F32, name="hgT%d" % k) for k in range(2)]
+        g_f32 = keep.tile([P, 2, T], F32, name="g_f32")
+        ha_words = keep.tile([P, 2, N, T], BF16, align_bytes=64, name="ha_words")
         ha_codes = keep.tile([P, 2, N], U32, align_bytes=64, name="ha_codes")
         ha_sc = keep.tile([P, 2, N], U8, align_bytes=64, name="ha_sc")
+        p_words = keep.tile([P, M, T], BF16, align_bytes=64, name="p_words")
         p_codes = keep.tile([P, M], U32, align_bytes=64, name="p_codes")
         p_sc = keep.tile([P, M], U8, align_bytes=64, name="p_sc")
 
-        pw = keep.tile([P, E], BF16, align_bytes=64, name="pw")
-        for j in range(4):
+        p_rows = keep.tile([P, E], BF16, align_bytes=64, name="p_rows")
+        for b in range(E // 128):
+            cols = slice(128 * b, 128 * b + 128)
             nc.vector.tensor_scalar(
-                out=pw[:, 128 * j : 128 * j + 128], in0=pb_sb[:, 128 * j : 128 * j + 128].bitcast(FP8),
-                scalar1=ps_sb[:, j : j + 1], scalar2=None, op0=ALU.mult,
+                out=p_rows[:, cols], in0=p_bytes_sb[:, cols].bitcast(FP8), scalar1=p_scale_sb[:, b : b + 1],
+                scalar2=None, op0=ALU.mult,
             )
-        h_words = h_sb[:].bitcast(F32)
-        for k in range(2):
-            xt = banks.tile([P, 2, N], F32, name="bank")
+
+        def turn_words(rows_bf16, k):
+            words = rows_bf16.bitcast(F32)
+            turned = banks.tile([P, 2, P], F32, name="bank")
             for u in range(2):
-                nc.tensor.transpose(xt[:, u, :], h_words[:, 256 * k + u : 256 * (k + 1) : 2], ident[:])
-            pairs = xt[:].bitcast(BF16)
+                nc.tensor.transpose(turned[:, u, :], words[:, 256 * k + u : 256 * (k + 1) : 2], ident[:])
+            return turned
+
+        for k in range(2):
+            pairs = turn_words(h_sb[:], k)[:].bitcast(BF16)
             nc.vector.tensor_tensor(
-                out=ha_grp[:, k].rearrange("p n (u e) -> p n u e", e=2),
+                out=ha_words[:, k].rearrange("p n (u e) -> p n u e", e=2),
                 in0=pairs.rearrange("p u (n e) -> p n u e", e=2),
                 in1=a_sb[:, k, :].rearrange("p (u e) -> p u e", e=2).unsqueeze(1).to_broadcast([P, N, 2, 2]),
                 op=ALU.mult,
@@ -121,166 +129,173 @@ def tile_segrnnparallelsegmentdecoder_d1p_kernel(
                 out=hT[k][:].rearrange("p (u e) n -> p u e n", e=2),
                 in_=pairs.rearrange("p u (n e) -> p u e n", e=2),
             )
-        p_words = pw[:].bitcast(F32)
-        xt = banks.tile([P, 2, N], F32, name="bank")
-        for u in range(2):
-            nc.tensor.transpose(xt[:, u, :], p_words[:, u:256:2], ident[:])
-        p_grp = keep.tile([P, M, 4], BF16, align_bytes=64, name="p_grp")
-        nc.vector.tensor_copy(out=p_grp[:].rearrange("p m t -> p (m t)").bitcast(F32).rearrange("p (m u) -> p m u", u=2),
-                              in_=xt[:].rearrange("p u m -> p m u"))
+        nc.vector.tensor_copy(
+            out=p_words[:].rearrange("p m t -> p (m t)").bitcast(F32).rearrange("p (m u) -> p m u", u=2),
+            in_=turn_words(p_rows[:], 0)[:].rearrange("p u m -> p m u"),
+        )
         nc.vector.quantize_mx(
             out=ha_codes[:].rearrange("p k n -> p (k n)").bitcast(FP8X4),
             scales=ha_sc[:].rearrange("p k n -> p (k n)"),
-            in_=ha_grp[:].rearrange("p k n t -> p (k n t)"),
+            in_=ha_words[:].rearrange("p k n t -> p (k n t)"),
         )
-        nc.vector.tensor_copy(out=gF[:], in_=g_sb[:])
-        nc.vector.quantize_mx(out=p_codes[:].bitcast(FP8X4), scales=p_sc[:], in_=p_grp[:].rearrange("p m t -> p (m t)"))
+        nc.vector.tensor_copy(out=g_f32[:], in_=g_sb[:])
+        nc.vector.quantize_mx(
+            out=p_codes[:].bitcast(FP8X4), scales=p_sc[:], in_=p_words[:].rearrange("p m t -> p (m t)")
+        )
         for k in range(2):
             nc.vector.tensor_tensor(
-                out=hgT[k][:], in0=hT[k][:], in1=gF[:, k, :].unsqueeze(2).to_broadcast([P, 4, N]), op=ALU.mult
+                out=hgT[k][:], in0=hT[k][:], in1=g_f32[:, k, :].unsqueeze(2).to_broadcast([P, T, N]), op=ALU.mult
             )
 
-        ur = [keep.tile([P, 4, N], F32, name="ur%d" % k) for k in range(2)]
-        un = [keep.tile([P, 4, N], F32, name="un%d" % k) for k in range(2)]
-        vr = [keep.tile([P, 4, M], F32, name="vr%d" % k) for k in range(2)]
-        vz_row = {}
-        park = out[N - NB : N].rearrange("n m w -> (n m w)").rearrange("(k n c) -> k n c", k=2, c=512)
-        vn = [vbank.tile([P, 4, M], F32, name="vn%d" % k) for k in range(2)]
-
+        ur = [keep.tile([P, T, N], F32, name="ur%d" % k) for k in range(2)]
+        minus_uz = [keep.tile([P, T, N], F32, name="minus_uz%d" % k) for k in range(2)]
+        un = [keep.tile([P, T, N], F32, name="un%d" % k) for k in range(2)]
+        vr = [keep.tile([P, T, M], F32, name="vr%d" % k) for k in range(2)]
+        vz = [keep.tile([P, T, M], F32, name="vz%d" % k) for k in range(2)]
+        vz_rows = [keep.tile([P, T, P], F32, name="vz_rows%d" % k) for k in range(2)]
+        vn = [vn_banks.tile([P, T, M], F32, name="vn%d" % k) for k in range(2)]
         rows = {}
+        park = out[N - NB : N].rearrange("n m w -> (n m w)").rearrange("(k n c) -> k n c", k=2, c=HALF)
 
-        def multiply(k, q):
-            acc = banks.tile([P, 512], F32, name="bank")
+        def project(k, q):
+            cols = slice(H * q + HALF * k, H * q + HALF * k + HALF)
+            u_bank = banks.tile([P, HALF], F32, name="bank")
             for c in range(2):
                 nc.tensor.matmul_mx(
-                    out=acc[:], lhsT=ha_codes[:, c, :].bitcast(FP8X4), lhsT_scale=ha_sc[:, c, :],
-                    rhs=wh_sb[k, q][:, c, :].bitcast(FP4X4),
-                    rhs_scale=wh_sc[:, c, H * q + 512 * k : H * q + 512 * k + 512],
+                    out=u_bank[:], lhsT=ha_codes[:, c, :].bitcast(FP8X4), lhsT_scale=ha_sc[:, c, :],
+                    rhs=wh_sb[k, q][:, c, :].bitcast(FP4X4), rhs_scale=wh_sc[:, c, cols],
                     start=(c == 0), stop=(c == 1),
                 )
-            u_row = head.tile([P, 4, P], F32, name="u_row")
-            nc.vector.tensor_copy(out=u_row[:], in_=acc[:].rearrange("n (p t) -> n t p", t=4))
-            acc = banks.tile([P, 512], F32, name="bank")
+            u_rows = head.tile([P, T, P], F32, name="u_rows")
+            nc.vector.tensor_copy(out=u_rows[:], in_=u_bank[:].rearrange("n (p t) -> n t p", t=T))
+            if q == Z_GATE:
+                nc.sync.dma_start(out=park[k], in_=u_rows[:].rearrange("n t p -> n (t p)"))
+            v_bank = banks.tile([P, HALF], F32, name="bank")
             nc.tensor.matmul_mx(
-                out=acc[:], lhsT=p_codes[:].bitcast(FP8X4), lhsT_scale=p_sc[:],
-                rhs=wi_sb[k, q][:].bitcast(FP4X4),
-                rhs_scale=wi_sc[:, H * q + 512 * k : H * q + 512 * k + 512],
-                start=True, stop=True,
+                out=v_bank[:], lhsT=p_codes[:].bitcast(FP8X4), lhsT_scale=p_sc[:],
+                rhs=wi_sb[k, q][:].bitcast(FP4X4), rhs_scale=wi_sc[:, cols], start=True, stop=True,
             )
-            if q == 1:
-                nc.sync.dma_start(out=park[k], in_=u_row[:].rearrange("n t p -> n (t p)"))
-                v_row = keep.tile([P, 4, P], F32, name="vz_row%d" % k)
-                vz_row[k] = v_row
-            else:
-                v_row = head.tile([P, 4, P], F32, name="v_row")
-            nc.scalar.copy(out=v_row[:], in_=acc[:].rearrange("n (p t) -> n t p", t=4))
-            rows[k, q] = (u_row, v_row)
+            v_rows = vz_rows[k] if q == Z_GATE else head.tile([P, T, P], F32, name="v_rows")
+            nc.scalar.copy(out=v_rows[:], in_=v_bank[:].rearrange("m (p t) -> m t p", t=T))
+            rows[k, q] = (u_rows, v_rows)
 
         def turn(k, q):
-            u_row, v_row = rows[k, q]
-            xu = banks.tile([P, 4, N], F32, name="bank")
-            for t in range(4):
-                nc.tensor.transpose(xu[:, t, :], u_row[:, t, :], ident[:])
-            nc.vector.tensor_copy(out=(ur[k] if q == 0 else un[k])[:], in_=xu[:])
-            xv = vn[k] if q == 2 else banks.tile([P, 4, M], F32, name="bank")
-            for t in range(4):
-                nc.tensor.transpose(xv[:, t, :], v_row[:, t, :], ident[:])
-            if q == 0:
-                nc.scalar.copy(out=vr[k][:], in_=xv[:])
+            u_rows, v_rows = rows[k, q]
+            u_turned = banks.tile([P, T, N], F32, name="bank")
+            for t in range(T):
+                nc.tensor.transpose(u_turned[:, t, :], u_rows[:, t, :], ident[:])
+            if q == Z_GATE:
+                nc.vector.tensor_scalar(
+                    out=minus_uz[k][:], in0=u_turned[:], scalar1=-1.0, scalar2=None, op0=ALU.mult
+                )
+            else:
+                nc.vector.tensor_copy(out=(ur if q == R_GATE else un)[k][:], in_=u_turned[:])
+            v_turned = vn[k] if q == N_GATE else banks.tile([P, T, M], F32, name="bank")
+            for t in range(T):
+                nc.tensor.transpose(v_turned[:, t, :], v_rows[:, t, :], ident[:])
+            if q != N_GATE:
+                nc.scalar.copy(out=(vr if q == R_GATE else vz)[k][:], in_=v_turned[:])
 
-        units = 2 * (N // NB)
         live = {}
+        whole, parts = slice(0, NB), (slice(0, 2), slice(2, NB))
 
-        def lanes():
-            return [(t, i) for i in range(NB) for t in range(4)]
+        def place(j):
+            return j % 2, NB * (j // 2)
+
+        def gate_by_bias(j, v, u_col, scale, name):
+            k, n0 = place(j)
+            gate = work.tile([P, T, NB, M], F32, bufs=3, name=name)
+            for i in range(NB):
+                for t in range(T):
+                    nc.scalar.activation(
+                        out=gate[:, t, i, :], in_=v[k][:, t, :], func=ACT.Sigmoid,
+                        bias=u_col[k][:, t, n0 + i : n0 + i + 1], scale=scale,
+                    )
+            live[name, j] = gate
 
         def gate_r(j):
-            kg, n0 = j % 2, NB * (j // 2)
-            r = work.tile([P, 4, NB, M], F32, bufs=3, name="r")
-            for t, i in lanes():
-                nc.scalar.activation(out=r[:, t, i, :], in_=vr[kg][:, t, :], func=ACT.Sigmoid,
-                                     bias=ur[kg][:, t, n0 + i : n0 + i + 1])
-            live["r", j] = r
+            gate_by_bias(j, vr, ur, 1.0, "r")
 
-        def spread(j):
-            kg, n0 = j % 2, NB * (j // 2)
-            uz = work.tile([P, NB, 4, P], F32, bufs=3, name="uz")
+        def spread_uz(j):
+            k, n0 = place(j)
+            uz = work.tile([P, NB, T, P], F32, bufs=3, name="uz")
             nc.sync.dma_start(
                 out=uz[:].rearrange("m i t p -> m (i t p)"),
-                in_=park[kg, n0 : n0 + NB, :].rearrange("n c -> (n c)").partition_broadcast(P),
+                in_=park[k, n0 : n0 + NB, :].rearrange("n c -> (n c)").partition_broadcast(P),
             )
             live["uz", j] = uz
 
         def sum_z(j):
-            kg = j % 2
-            uz = live["uz", j]
+            k = j % 2
             sums = []
             for i in range(NB):
-                bank = banks.tile([P, 4, M], F32, name="bank")
-                for t in range(4):
-                    nc.tensor.matmul(bank[:, t, :], lhsT=vz_row[kg][:, t, :], rhs=ident[:], start=True, stop=False, is_transpose=True)
-                    nc.tensor.matmul(bank[:, t, :], lhsT=uz[:, i, t, :], rhs=ident[:], start=False, stop=True, is_transpose=True)
-                sums.append(bank)
-            live["xz", j] = sums
+                z_sum = banks.tile([P, T, M], F32, name="bank")
+                for t in range(T):
+                    nc.tensor.matmul(
+                        z_sum[:, t, :], lhsT=vz_rows[k][:, t, :], rhs=ident[:], start=True, stop=False, is_transpose=True
+                    )
+                    nc.tensor.matmul(
+                        z_sum[:, t, :], lhsT=live["uz", j][:, i, t, :], rhs=ident[:], start=False, stop=True,
+                        is_transpose=True,
+                    )
+                sums.append(z_sum)
+            live["z_sum", j] = sums
 
         def gate_z(j):
-            z = work.tile([P, 4, NB, M], F32, bufs=3, name="z")
-            for i in range(NB):
-                nc.scalar.activation(out=z[:, :, i, :], in_=live["xz", j][i][:], func=ACT.Sigmoid, scale=-1.0)
-            live["z", j] = z
+            if j < 2:
+                gate_by_bias(j, vz, minus_uz, -1.0, "zc")
+            else:
+                zc = work.tile([P, T, NB, M], F32, bufs=3, name="zc")
+                for i in range(NB):
+                    nc.scalar.activation(out=zc[:, :, i, :], in_=live["z_sum", j][i][:], func=ACT.Sigmoid, scale=-1.0)
+                live["zc", j] = zc
 
-        def pre_candidate(j, part):
-            kg, n0 = j % 2, NB * (j // 2)
-            if part == 0:
-                s = work.tile([P, 4, NB, M], F32, bufs=2, name="s")
-                live["s", j] = s
-            s = live["s", j]
-            r = live["r", j]
-            for t, i in lanes()[8 * part : 8 * part + 8]:
-                nc.vector.scalar_tensor_tensor(
-                    out=s[:, t, i, :], in0=r[:, t, i, :], scalar=un[kg][:, t, n0 + i : n0 + i + 1],
-                    in1=vn[kg][:, t, :], op0=ALU.mult, op1=ALU.add,
-                )
+        def pre_candidate(j):
+            k, n0 = place(j)
+            x = work.tile([P, T, NB, M], F32, name="x")
+            for i in range(NB):
+                for t in range(T):
+                    nc.vector.scalar_tensor_tensor(
+                        out=x[:, t, i, :], in0=live["r", j][:, t, i, :], scalar=un[k][:, t, n0 + i : n0 + i + 1],
+                        in1=vn[k][:, t, :], op0=ALU.mult, op1=ALU.add,
+                    )
+            live["x", j] = x
 
         def candidate(j, cut):
             if cut.start == 0:
-                c = work.tile([P, 4, NB, M], F32, bufs=2, name="c")
-                live["c", j] = c
-            nc.scalar.activation(out=live["c", j][:, :, cut, :], in_=live["s", j][:, :, cut, :], func=ACT.Tanh)
+                live["c", j] = work.tile([P, T, NB, M], F32, name="c")
+            nc.scalar.activation(out=live["c", j][:, :, cut, :], in_=live["x", j][:, :, cut, :], func=ACT.Tanh)
 
         def mix(j, cut):
-            kg, n0 = j % 2, NB * (j // 2)
+            k, n0 = place(j)
             if cut.start == 0:
-                d = work.tile([P, 4, NB, M], F32, bufs=2, name="d")
-                live["d", j] = d
-            d, c, z = live["d", j], live["c", j], live["z", j]
+                live["d", j] = work.tile([P, T, NB, M], F32, name="d")
             for i in range(cut.start, cut.stop):
-                for t in range(4):
+                for t in range(T):
                     nc.vector.scalar_tensor_tensor(
-                        out=d[:, t, i, :], in0=c[:, t, i, :], scalar=hT[kg][:, t, n0 + i : n0 + i + 1],
-                        in1=z[:, t, i, :], op0=ALU.subtract, op1=ALU.mult,
+                        out=live["d", j][:, t, i, :], in0=live["c", j][:, t, i, :],
+                        scalar=hT[k][:, t, n0 + i : n0 + i + 1], in1=live["zc", j][:, t, i, :],
+                        op0=ALU.subtract, op1=ALU.mult,
                     )
 
         def gain(j, cut):
-            kg, n0 = j % 2, NB * (j // 2)
+            k, n0 = place(j)
             if cut.start == 0:
-                sg = work.tile([P, 4, NB * M], BF16, bufs=2, align_bytes=64, name="sg")
-                live["sg", j] = sg
-            sg, d = live["sg", j], live["d", j]
+                live["sg", j] = work.tile([P, T, NB * M], BF16, align_bytes=64, name="sg")
             for i in range(cut.start, cut.stop):
-                for t in range(4):
+                for t in range(T):
                     nc.vector.tensor_scalar(
-                        out=sg[:, t, M * i : M * i + M], in0=d[:, t, i, :], scalar1=gF[:, kg, t : t + 1],
-                        scalar2=hgT[kg][:, t, n0 + i : n0 + i + 1], op0=ALU.mult, op1=ALU.add,
+                        out=live["sg", j][:, t, M * i : M * i + M], in0=live["d", j][:, t, i, :],
+                        scalar1=g_f32[:, k, t : t + 1], scalar2=hgT[k][:, t, n0 + i : n0 + i + 1],
+                        op0=ALU.mult, op1=ALU.add,
                     )
 
         def interleave(j, cut):
             if cut.start == 0:
-                grp = work.tile([P, NB * M, 4], BF16, bufs=2, align_bytes=64, name="grp")
-                live["grp", j] = grp
+                live["sg_words", j] = work.tile([P, NB * M, T], BF16, align_bytes=64, name="sg_words")
             cols = slice(M * cut.start, M * cut.stop)
-            dst, src = live["grp", j][:, cols, :], live["sg", j][:, :, cols]
-            if j >= units - 2:
+            dst, src = live["sg_words", j][:, cols, :], live["sg", j][:, :, cols]
+            if j >= UNITS - 2:
                 nc.vector.tensor_copy(
                     out=dst.rearrange("p (c i) t -> p c t i", i=4), in_=src.rearrange("p t (c i) -> p c t i", i=4)
                 )
@@ -298,104 +313,95 @@ def tile_segrnnparallelsegmentdecoder_d1p_kernel(
             cols = slice(M * cut.start, M * cut.stop)
             nc.vector.quantize_mx(
                 out=codes[:, cols].bitcast(FP8X4), scales=scales[:, cols],
-                in_=live["grp", j][:, cols, :].rearrange("p c t -> p (c t)"),
+                in_=live["sg_words", j][:, cols, :].rearrange("p c t -> p (c t)"),
             )
 
-        def project_out(b, cut):
-            for half in range(cut.start // 2, cut.stop // 2):
-                acc = out_banks.tile([P, 2, W], F32, name="acc")
-                for i in range(2):
-                    rows_n = slice(M * (2 * half + i), M * (2 * half + i) + M)
-                    for w in range(2):
-                        for kg in range(2):
-                            codes, scales = live["q", 2 * b + kg]
-                            nc.tensor.matmul_mx(
-                                out=acc[:, i, 128 * w : 128 * w + 128],
-                                lhsT=codes[:, rows_n].bitcast(FP8X4), lhsT_scale=scales[:, rows_n],
-                                rhs=wo_sb[:, kg, 256 * w : 256 * w + 256].bitcast(FP4X4),
-                                rhs_scale=wo_sc[:, kg, 128 * w : 128 * w + 128],
-                                start=(kg == 0), stop=(kg == 1),
-                            )
-                live["acc", b, half] = acc
+        def project_out(b, part):
+            acc = out_banks.tile([P, 2, W], F32, name="acc")
+            for i in range(2):
+                cols = slice(M * (2 * part + i), M * (2 * part + i + 1))
+                for w in range(2):
+                    for k in range(2):
+                        codes, scales = live["q", 2 * b + k]
+                        nc.tensor.matmul_mx(
+                            out=acc[:, i, 128 * w : 128 * w + 128],
+                            lhsT=codes[:, cols].bitcast(FP8X4), lhsT_scale=scales[:, cols],
+                            rhs=wo_sb[:, k, 256 * w : 256 * w + 256].bitcast(FP4X4),
+                            rhs_scale=wo_sc[:, k, 128 * w : 128 * w + 128],
+                            start=(k == 0), stop=(k == 1),
+                        )
+            live["acc", b, part] = acc
 
-        def empty(b, half):
-            if half == 0:
-                o_sb = work.tile([P, NB, W], F32, bufs=3, name="o_sb")
-                live["o", b] = o_sb
-            part = slice(2 * half, 2 * half + 2)
-            nc.vector.tensor_copy(out=live["o", b][:, part, :], in_=live["acc", b, half][:])
-            if half == 1:
-                nc.sync.dma_start(out=out[NB * b : NB * b + NB].rearrange("n m w -> m n w"), in_=live["o", b][:])
-
-        whole, halves = [slice(0, NB)], [slice(0, 2), slice(2, NB)]
-
-        multiply(0, 1)
-        spread(0)
-        multiply(0, 0)
-        turn(0, 0)
-        gate_r(0)
-        multiply(0, 2)
-        turn(0, 2)
-        multiply(1, 1)
-        spread(1)
-        pre_candidate(0, 0)
-        pre_candidate(0, 1)
-        multiply(1, 0)
-        turn(1, 0)
-        gate_r(1)
-        candidate(0, whole[0])
-        multiply(1, 2)
-        turn(1, 2)
-        sum_z(0)
-        gate_z(0)
-        pre_candidate(1, 0)
-        pre_candidate(1, 1)
-        spread(2)
-        sum_z(1)
-        gate_r(2)
-        for j in range(1, units):
-            gate_z(j)
-            for cut in whole if j < units - 1 else halves:
-                candidate(j, cut)
-            if j + 2 < units:
-                gate_r(j + 2)
-                spread(j + 2)
-            if j + 1 < units:
-                sum_z(j + 1)
-            mix(j - 1, whole[0])
-            if j >= 2:
-                quantize(j - 2, whole[0])
-            gain(j - 1, whole[0])
-            interleave(j - 1, whole[0])
-            if j + 1 < units:
-                pre_candidate(j + 1, 0)
-            if j >= 4:
-                empty((j - 4) // 2, j % 2)
-            if j + 1 < units:
-                pre_candidate(j + 1, 1)
-            if j >= 3:
-                project_out((j - 3) // 2, halves[(j - 3) % 2])
-
-        last, b = units - 1, N // NB - 1
-        o_sb = work.tile([P, NB, W], F32, bufs=3, name="o_sb")
-        mix(last, halves[0])
-        quantize(last - 1, whole[0])
-        empty(b - 1, 0)
-        project_out(b - 1, halves[1])
-        gain(last, halves[0])
-        mix(last, halves[1])
-        interleave(last, halves[0])
-        quantize(last, halves[0])
-        project_out(b, halves[0])
-        gain(last, halves[1])
-        empty(b - 1, 1)
-        interleave(last, halves[1])
-        quantize(last, halves[1])
-        project_out(b, halves[1])
-        for half in range(2):
-            part = slice(2 * half, 2 * half + 2)
-            copy_out = nc.scalar.copy if half == 0 else nc.vector.tensor_copy
-            copy_out(out=o_sb[:, part, :], in_=live["acc", b, half][:])
+        def store(b, part):
+            if part == 0:
+                live["o", b] = work.tile([P, NB, W], F32, name="o")
+            copy_out = nc.scalar.copy if part == 0 else nc.vector.tensor_copy
+            copy_out(out=live["o", b][:, 2 * part : 2 * part + 2, :], in_=live["acc", b, part][:])
+            n0 = NB * b + 2 * part
             nc.sync.dma_start(
-                out=out[NB * b + 2 * half : NB * b + 2 * half + 2].rearrange("n m w -> m n w"), in_=o_sb[:, part, :]
+                out=out[n0 : n0 + 2].rearrange("n m w -> m n w"), in_=live["o", b][:, 2 * part : 2 * part + 2, :]
             )
+
+        project(0, R_GATE)
+        turn(0, R_GATE)
+        gate_r(0)
+        project(0, Z_GATE)
+        project(0, N_GATE)
+        turn(0, Z_GATE)
+        turn(0, N_GATE)
+        pre_candidate(0)
+        gate_z(0)
+        candidate(0, whole)
+        project(1, R_GATE)
+        turn(1, R_GATE)
+        gate_r(1)
+        project(1, Z_GATE)
+        project(1, N_GATE)
+        turn(1, Z_GATE)
+        turn(1, N_GATE)
+        spread_uz(2)
+        spread_uz(3)
+        pre_candidate(1)
+        gate_r(2)
+
+        for j in range(1, UNITS):
+            gate_z(j)
+            for cut in (whole,) if j < UNITS - 1 else parts:
+                candidate(j, cut)
+            if j >= 4 and j % 2 == 0:
+                store(j // 2 - 2, 0)
+            if j + 2 < UNITS:
+                gate_r(j + 2)
+            if j + 3 < UNITS:
+                spread_uz(j + 3)
+            if j + 1 < UNITS:
+                sum_z(j + 1)
+            mix(j - 1, whole)
+            gain(j - 1, whole)
+            interleave(j - 1, whole)
+            if j >= 2:
+                quantize(j - 2, whole)
+            if j + 1 < UNITS:
+                pre_candidate(j + 1)
+            if j >= 5 and j % 2 == 1:
+                store(j // 2 - 2, 1)
+            if j >= 3:
+                project_out((j - 3) // 2, (j - 3) % 2)
+
+        last, b = UNITS - 1, N // NB - 1
+        mix(last, parts[0])
+        quantize(last - 1, whole)
+        store(b - 1, 0)
+        project_out(b - 1, 1)
+        gain(last, parts[0])
+        mix(last, parts[1])
+        interleave(last, parts[0])
+        quantize(last, parts[0])
+        project_out(b, 0)
+        gain(last, parts[1])
+        store(b - 1, 1)
+        interleave(last, parts[1])
+        quantize(last, parts[1])
+        project_out(b, 1)
+        store(b, 0)
+        store(b, 1)

from contextlib import ExitStack

import concourse.mybir as mybir
from concourse.masks import make_identity

N, M, E, H, W = 128, 128, 512, 1024, 256
P = 128
T = 4
HALF = P * T
R_GATE, Z_GATE, N_GATE = 0, 1, 2
NB = 4
UNITS = 2 * N // NB
FLOPS = 2 * N * H * 3 * H + 2 * M * E * 3 * H + 2 * N * M * H * W

F32 = mybir.dt.float32
BF16 = mybir.dt.bfloat16
I32 = mybir.dt.int32
U32 = mybir.dt.uint32
U8 = mybir.dt.uint8
FP8 = mybir.dt.float8_e4m3fn
FP8X4 = mybir.dt.float8_e4m3fn_x4
FP4X4 = mybir.dt.float4_e2m1fn_x4
ALU = mybir.AluOpType
ACT = mybir.ActivationFunctionType


def tile_segrnnparallelsegmentdecoder_d1p_kernel(
    tc, h, a, wh_words, wh_scales, p_bytes, p_scale, wi_words, wi_scales, g, wo_words, wo_scales, out
):
    nc = tc.nc
    with ExitStack() as ctx:
        keep = ctx.enter_context(tc.tile_pool(name="keep", bufs=1))
        head = ctx.enter_context(tc.tile_pool(name="head", bufs=3))
        work = ctx.enter_context(tc.tile_pool(name="work", bufs=2))
        vn_banks = ctx.enter_context(tc.psum_pool(name="vn_banks", bufs=1))
        banks = ctx.enter_context(tc.psum_pool(name="banks", bufs=4))
        out_banks = ctx.enter_context(tc.psum_pool(name="out_banks", bufs=2))
        ctx.enter_context(tc.manual_schedule())

        a_sb = keep.tile([P, 2, T], BF16, name="a_sb")
        nc.scalar.dma_start(out=a_sb[:], in_=a.rearrange("(g p t) -> p g t", g=2, t=T))
        p_scale_sb = keep.tile([P, E // 128], F32, name="p_scale_sb")
        nc.scalar.dma_start(out=p_scale_sb[:], in_=p_scale)
        g_sb = keep.tile([P, 2, T], BF16, name="g_sb")
        nc.scalar.dma_start(out=g_sb[:], in_=g.rearrange("(g p t) -> p g t", g=2, t=T))

        wh_sc = keep.tile([P, 2, 3 * H], U8, align_bytes=64, name="wh_sc")
        wi_sc = keep.tile([P, 3 * H], U8, align_bytes=64, name="wi_sc")
        wo_sc = keep.tile([P, 2, W], U8, align_bytes=64, name="wo_sc")
        for plane in (wh_sc, wi_sc, wo_sc):
            nc.vector.memset(plane[:].bitcast(I32), 0)

        wh_sb, wi_sb = {}, {}

        def load_words(k, q):
            cols = slice((q * H + k * HALF) // 2, (q * H + (k + 1) * HALF) // 2)
            wh_sb[k, q] = keep.tile([P, 2, 2 * HALF], U8, align_bytes=64, name="wh_sb%d%d" % (k, q))
            nc.sync.dma_start(
                out=wh_sb[k, q][:].bitcast(I32), in_=wh_words.bitcast(I32)[:, :, cols].rearrange("g p w -> p g w")
            )
            wi_sb[k, q] = keep.tile([P, 2 * HALF], U8, align_bytes=64, name="wi_sb%d%d" % (k, q))
            nc.sync.dma_start(out=wi_sb[k, q][:].bitcast(I32), in_=wi_words[0].bitcast(I32)[:, cols])

        h_sb = keep.tile([P, H], BF16, align_bytes=64, name="h_sb")
        nc.sync.dma_start(out=h_sb[:], in_=h)
        p_bytes_sb = keep.tile([P, E], U8, align_bytes=64, name="p_bytes_sb")
        nc.sync.dma_start(out=p_bytes_sb[:], in_=p_bytes)
        load_words(0, R_GATE)
        for q in range(4):
            nc.sync.dma_start(
                out=wh_sc[32 * q : 32 * q + 4].bitcast(I32),
                in_=wh_scales[:, 4 * q : 4 * q + 4, :].rearrange("g q n -> q g n").bitcast(I32),
            )
        for q in range(4):
            nc.sync.dma_start(
                out=wi_sc[32 * q : 32 * q + 4, :].bitcast(I32), in_=wi_scales[0, 4 * q : 4 * q + 4, :].bitcast(I32)
            )
        for k, q in ((0, Z_GATE), (0, N_GATE), (1, R_GATE), (1, Z_GATE), (1, N_GATE)):
            load_words(k, q)
        wo_sb = keep.tile([P, 2, 2 * W], U8, align_bytes=64, name="wo_sb")
        nc.sync.dma_start(out=wo_sb[:].bitcast(I32), in_=wo_words.rearrange("g p w -> p g w").bitcast(I32))
        for q in range(4):
            nc.sync.dma_start(
                out=wo_sc[32 * q : 32 * q + 4].bitcast(I32),
                in_=wo_scales[:, 4 * q : 4 * q + 4, :].rearrange("g q n -> q g n").bitcast(I32),
            )

        warm = keep.tile([P, 1], F32, name="warm")
        nc.vector.memset(warm[:], 0.0)
        nc.scalar.activation(out=warm[:], in_=warm[:], func=ACT.Sigmoid)

        ident = keep.tile([P, P], F32, name="ident")
        make_identity(nc, ident[:])

        hT = [keep.tile([P, T, N], F32, name="hT%d" % k) for k in range(2)]
        hgT = [keep.tile([P, T, N], F32, name="hgT%d" % k) for k in range(2)]
        g_f32 = keep.tile([P, 2, T], F32, name="g_f32")
        ha_words = keep.tile([P, 2, N, T], BF16, align_bytes=64, name="ha_words")
        ha_codes = keep.tile([P, 2, N], U32, align_bytes=64, name="ha_codes")
        ha_sc = keep.tile([P, 2, N], U8, align_bytes=64, name="ha_sc")
        p_words = keep.tile([P, M, T], BF16, align_bytes=64, name="p_words")
        p_codes = keep.tile([P, M], U32, align_bytes=64, name="p_codes")
        p_sc = keep.tile([P, M], U8, align_bytes=64, name="p_sc")

        p_rows = keep.tile([P, E], BF16, align_bytes=64, name="p_rows")
        for b in range(E // 128):
            cols = slice(128 * b, 128 * b + 128)
            nc.vector.tensor_scalar(
                out=p_rows[:, cols], in0=p_bytes_sb[:, cols].bitcast(FP8), scalar1=p_scale_sb[:, b : b + 1],
                scalar2=None, op0=ALU.mult,
            )

        def turn_words(rows_bf16, k):
            words = rows_bf16.bitcast(F32)
            turned = banks.tile([P, 2, P], F32, name="bank")
            for u in range(2):
                nc.tensor.transpose(turned[:, u, :], words[:, 256 * k + u : 256 * (k + 1) : 2], ident[:])
            return turned

        for k in range(2):
            pairs = turn_words(h_sb[:], k)[:].bitcast(BF16)
            nc.vector.tensor_tensor(
                out=ha_words[:, k].rearrange("p n (u e) -> p n u e", e=2),
                in0=pairs.rearrange("p u (n e) -> p n u e", e=2),
                in1=a_sb[:, k, :].rearrange("p (u e) -> p u e", e=2).unsqueeze(1).to_broadcast([P, N, 2, 2]),
                op=ALU.mult,
            )
            nc.scalar.copy(
                out=hT[k][:].rearrange("p (u e) n -> p u e n", e=2),
                in_=pairs.rearrange("p u (n e) -> p u e n", e=2),
            )
        nc.vector.tensor_copy(
            out=p_words[:].rearrange("p m t -> p (m t)").bitcast(F32).rearrange("p (m u) -> p m u", u=2),
            in_=turn_words(p_rows[:], 0)[:].rearrange("p u m -> p m u"),
        )
        nc.vector.quantize_mx(
            out=ha_codes[:].rearrange("p k n -> p (k n)").bitcast(FP8X4),
            scales=ha_sc[:].rearrange("p k n -> p (k n)"),
            in_=ha_words[:].rearrange("p k n t -> p (k n t)"),
        )
        nc.vector.tensor_copy(out=g_f32[:], in_=g_sb[:])
        nc.vector.quantize_mx(
            out=p_codes[:].bitcast(FP8X4), scales=p_sc[:], in_=p_words[:].rearrange("p m t -> p (m t)")
        )
        for k in range(2):
            nc.vector.tensor_tensor(
                out=hgT[k][:], in0=hT[k][:], in1=g_f32[:, k, :].unsqueeze(2).to_broadcast([P, T, N]), op=ALU.mult
            )

        ur = [keep.tile([P, T, N], F32, name="ur%d" % k) for k in range(2)]
        minus_uz = [keep.tile([P, T, N], F32, name="minus_uz%d" % k) for k in range(2)]
        un = [keep.tile([P, T, N], F32, name="un%d" % k) for k in range(2)]
        vr = [keep.tile([P, T, M], F32, name="vr%d" % k) for k in range(2)]
        vz = [keep.tile([P, T, M], F32, name="vz%d" % k) for k in range(2)]
        vz_rows = [keep.tile([P, T, P], F32, name="vz_rows%d" % k) for k in range(2)]
        vn = [vn_banks.tile([P, T, M], F32, name="vn%d" % k) for k in range(2)]
        rows = {}
        park = out[N - NB : N].rearrange("n m w -> (n m w)").rearrange("(k n c) -> k n c", k=2, c=HALF)

        def project(k, q):
            cols = slice(H * q + HALF * k, H * q + HALF * k + HALF)
            u_bank = banks.tile([P, HALF], F32, name="bank")
            for c in range(2):
                nc.tensor.matmul_mx(
                    out=u_bank[:], lhsT=ha_codes[:, c, :].bitcast(FP8X4), lhsT_scale=ha_sc[:, c, :],
                    rhs=wh_sb[k, q][:, c, :].bitcast(FP4X4), rhs_scale=wh_sc[:, c, cols],
                    start=(c == 0), stop=(c == 1),
                )
            u_rows = head.tile([P, T, P], F32, name="u_rows")
            nc.vector.tensor_copy(out=u_rows[:], in_=u_bank[:].rearrange("n (p t) -> n t p", t=T))
            if q == Z_GATE:
                nc.sync.dma_start(out=park[k], in_=u_rows[:].rearrange("n t p -> n (t p)"))
            v_bank = banks.tile([P, HALF], F32, name="bank")
            nc.tensor.matmul_mx(
                out=v_bank[:], lhsT=p_codes[:].bitcast(FP8X4), lhsT_scale=p_sc[:],
                rhs=wi_sb[k, q][:].bitcast(FP4X4), rhs_scale=wi_sc[:, cols], start=True, stop=True,
            )
            v_rows = vz_rows[k] if q == Z_GATE else head.tile([P, T, P], F32, name="v_rows")
            nc.scalar.copy(out=v_rows[:], in_=v_bank[:].rearrange("m (p t) -> m t p", t=T))
            rows[k, q] = (u_rows, v_rows)

        def turn(k, q):
            u_rows, v_rows = rows[k, q]
            u_turned = banks.tile([P, T, N], F32, name="bank")
            for t in range(T):
                nc.tensor.transpose(u_turned[:, t, :], u_rows[:, t, :], ident[:])
            if q == Z_GATE:
                nc.vector.tensor_scalar(
                    out=minus_uz[k][:], in0=u_turned[:], scalar1=-1.0, scalar2=None, op0=ALU.mult
                )
            else:
                nc.vector.tensor_copy(out=(ur if q == R_GATE else un)[k][:], in_=u_turned[:])
            v_turned = vn[k] if q == N_GATE else banks.tile([P, T, M], F32, name="bank")
            for t in range(T):
                nc.tensor.transpose(v_turned[:, t, :], v_rows[:, t, :], ident[:])
            if q != N_GATE:
                nc.scalar.copy(out=(vr if q == R_GATE else vz)[k][:], in_=v_turned[:])

        live = {}
        whole, parts = slice(0, NB), (slice(0, 2), slice(2, NB))

        def place(j):
            return j % 2, NB * (j // 2)

        def gate_by_bias(j, v, u_col, scale, name):
            k, n0 = place(j)
            gate = work.tile([P, T, NB, M], F32, bufs=3, name=name)
            for i in range(NB):
                for t in range(T):
                    nc.scalar.activation(
                        out=gate[:, t, i, :], in_=v[k][:, t, :], func=ACT.Sigmoid,
                        bias=u_col[k][:, t, n0 + i : n0 + i + 1], scale=scale,
                    )
            live[name, j] = gate

        def gate_r(j):
            gate_by_bias(j, vr, ur, 1.0, "r")

        def spread_uz(j):
            k, n0 = place(j)
            uz = work.tile([P, NB, T, P], F32, bufs=3, name="uz")
            nc.sync.dma_start(
                out=uz[:].rearrange("m i t p -> m (i t p)"),
                in_=park[k, n0 : n0 + NB, :].rearrange("n c -> (n c)").partition_broadcast(P),
            )
            live["uz", j] = uz

        def sum_z(j):
            k = j % 2
            sums = []
            for i in range(NB):
                z_sum = banks.tile([P, T, M], F32, name="bank")
                for t in range(T):
                    nc.tensor.matmul(
                        z_sum[:, t, :], lhsT=vz_rows[k][:, t, :], rhs=ident[:], start=True, stop=False, is_transpose=True
                    )
                    nc.tensor.matmul(
                        z_sum[:, t, :], lhsT=live["uz", j][:, i, t, :], rhs=ident[:], start=False, stop=True,
                        is_transpose=True,
                    )
                sums.append(z_sum)
            live["z_sum", j] = sums

        def gate_z(j):
            if j < 2:
                gate_by_bias(j, vz, minus_uz, -1.0, "zc")
            else:
                zc = work.tile([P, T, NB, M], F32, bufs=3, name="zc")
                for i in range(NB):
                    nc.scalar.activation(out=zc[:, :, i, :], in_=live["z_sum", j][i][:], func=ACT.Sigmoid, scale=-1.0)
                live["zc", j] = zc

        def pre_candidate(j):
            k, n0 = place(j)
            x = work.tile([P, T, NB, M], F32, name="x")
            for i in range(NB):
                for t in range(T):
                    nc.vector.scalar_tensor_tensor(
                        out=x[:, t, i, :], in0=live["r", j][:, t, i, :], scalar=un[k][:, t, n0 + i : n0 + i + 1],
                        in1=vn[k][:, t, :], op0=ALU.mult, op1=ALU.add,
                    )
            live["x", j] = x

        def candidate(j, cut):
            if cut.start == 0:
                live["c", j] = work.tile([P, T, NB, M], F32, name="c")
            nc.scalar.activation(out=live["c", j][:, :, cut, :], in_=live["x", j][:, :, cut, :], func=ACT.Tanh)

        def mix(j, cut):
            k, n0 = place(j)
            if cut.start == 0:
                live["d", j] = work.tile([P, T, NB, M], F32, name="d")
            for i in range(cut.start, cut.stop):
                for t in range(T):
                    nc.vector.scalar_tensor_tensor(
                        out=live["d", j][:, t, i, :], in0=live["c", j][:, t, i, :],
                        scalar=hT[k][:, t, n0 + i : n0 + i + 1], in1=live["zc", j][:, t, i, :],
                        op0=ALU.subtract, op1=ALU.mult,
                    )

        def gain(j, cut):
            k, n0 = place(j)
            if cut.start == 0:
                live["sg", j] = work.tile([P, T, NB * M], BF16, align_bytes=64, name="sg")
            for i in range(cut.start, cut.stop):
                for t in range(T):
                    nc.vector.tensor_scalar(
                        out=live["sg", j][:, t, M * i : M * i + M], in0=live["d", j][:, t, i, :],
                        scalar1=g_f32[:, k, t : t + 1], scalar2=hgT[k][:, t, n0 + i : n0 + i + 1],
                        op0=ALU.mult, op1=ALU.add,
                    )

        def interleave(j, cut):
            if cut.start == 0:
                live["sg_words", j] = work.tile([P, NB * M, T], BF16, align_bytes=64, name="sg_words")
            cols = slice(M * cut.start, M * cut.stop)
            dst, src = live["sg_words", j][:, cols, :], live["sg", j][:, :, cols]
            if j >= UNITS - 2:
                nc.vector.tensor_copy(
                    out=dst.rearrange("p (c i) t -> p c t i", i=4), in_=src.rearrange("p t (c i) -> p c t i", i=4)
                )
            else:
                nc.gpsimd.tensor_scalar(
                    out=dst, in0=src.rearrange("p t c -> p c t"), scalar1=1.0, scalar2=0.0, op0=ALU.mult, op1=ALU.add
                )

        def quantize(j, cut):
            if cut.start == 0:
                codes = work.tile([P, NB * M], U32, bufs=4, align_bytes=64, name="codes")
                scales = work.tile([P, NB * M], U8, bufs=4, align_bytes=64, name="scales")
                live["q", j] = (codes, scales)
            codes, scales = live["q", j]
            cols = slice(M * cut.start, M * cut.stop)
            nc.vector.quantize_mx(
                out=codes[:, cols].bitcast(FP8X4), scales=scales[:, cols],
                in_=live["sg_words", j][:, cols, :].rearrange("p c t -> p (c t)"),
            )

        def project_out(b, part):
            acc = out_banks.tile([P, 2, W], F32, name="acc")
            for i in range(2):
                cols = slice(M * (2 * part + i), M * (2 * part + i + 1))
                for w in range(2):
                    for k in range(2):
                        codes, scales = live["q", 2 * b + k]
                        nc.tensor.matmul_mx(
                            out=acc[:, i, 128 * w : 128 * w + 128],
                            lhsT=codes[:, cols].bitcast(FP8X4), lhsT_scale=scales[:, cols],
                            rhs=wo_sb[:, k, 256 * w : 256 * w + 256].bitcast(FP4X4),
                            rhs_scale=wo_sc[:, k, 128 * w : 128 * w + 128],
                            start=(k == 0), stop=(k == 1),
                        )
            live["acc", b, part] = acc

        def store(b, part):
            if part == 0:
                live["o", b] = work.tile([P, NB, W], F32, name="o")
            copy_out = nc.scalar.copy if part == 0 else nc.vector.tensor_copy
            copy_out(out=live["o", b][:, 2 * part : 2 * part + 2, :], in_=live["acc", b, part][:])
            n0 = NB * b + 2 * part
            nc.sync.dma_start(
                out=out[n0 : n0 + 2].rearrange("n m w -> m n w"), in_=live["o", b][:, 2 * part : 2 * part + 2, :]
            )

        project(0, R_GATE)
        turn(0, R_GATE)
        gate_r(0)
        project(0, Z_GATE)
        project(0, N_GATE)
        turn(0, Z_GATE)
        turn(0, N_GATE)
        pre_candidate(0)
        gate_z(0)
        candidate(0, whole)
        project(1, R_GATE)
        turn(1, R_GATE)
        gate_r(1)
        project(1, Z_GATE)
        project(1, N_GATE)
        turn(1, Z_GATE)
        turn(1, N_GATE)
        spread_uz(2)
        spread_uz(3)
        pre_candidate(1)
        gate_r(2)

        for j in range(1, UNITS):
            gate_z(j)
            for cut in (whole,) if j < UNITS - 1 else parts:
                candidate(j, cut)
            if j >= 4 and j % 2 == 0:
                store(j // 2 - 2, 0)
            if j + 2 < UNITS:
                gate_r(j + 2)
            if j + 3 < UNITS:
                spread_uz(j + 3)
            if j + 1 < UNITS:
                sum_z(j + 1)
            mix(j - 1, whole)
            gain(j - 1, whole)
            interleave(j - 1, whole)
            if j >= 2:
                quantize(j - 2, whole)
            if j + 1 < UNITS:
                pre_candidate(j + 1)
            if j >= 5 and j % 2 == 1:
                store(j // 2 - 2, 1)
            if j >= 3:
                project_out((j - 3) // 2, (j - 3) % 2)

        last, b = UNITS - 1, N // NB - 1
        mix(last, parts[0])
        quantize(last - 1, whole)
        store(b - 1, 0)
        project_out(b - 1, 1)
        gain(last, parts[0])
        mix(last, parts[1])
        interleave(last, parts[0])
        quantize(last, parts[0])
        project_out(b, 0)
        gain(last, parts[1])
        store(b - 1, 1)
        interleave(last, parts[1])
        quantize(last, parts[1])
        project_out(b, 1)
        store(b, 0)
        store(b, 1)
